import numpy as np, ml_dtypes
CORES = [51,54,179,182]
N = 4
BF = ml_dtypes.bfloat16
def f(rng, *shape):
    return (rng.standard_normal(shape, dtype=np.float32) * np.exp2(rng.integers(-2, 3, shape[:-1] + (1,)))).astype(BF)
def wide(rng, *shape):
    v = f(rng, *shape).astype(np.float32); k = shape[:-2] + (1, shape[-1])
    return (v * np.exp2(rng.integers(-6, 7, k)) * (rng.random(k) > 0.0625)).astype(BF)
W, V, L, DM, ST = 2048, 256, 256, 3, 6
def hotty(rng, hot, n, share):
    h = hot[np.arange(8)[None, :, None, None], rng.integers(0, hot.shape[1], (N, 8, 16, n))]
    return np.where(rng.random((N, 8, 16, n)) < share, h, rng.integers(0, W, (N, 8, 16, n)))
def parts(rng):
    hot = rng.integers(0, W, (8, W // 16)); share = rng.choice(np.array([0.25, 0.5, 0.75]), (N, 8, 1, 1))
    refs = hotty(rng, hot, V, share); gloss = hotty(rng, hot, W, share)
    u = rng.random((N, ST, L))
    need = np.where(u < 0.4, rng.integers(1, 45, u.shape), np.where(u < 0.9, rng.integers(58, 71, u.shape), rng.integers(90, 129, u.shape)))
    v = rng.integers(0, V, (N, 8, L)); p = rng.integers(0, V, (N, DM, 8, L)); a = rng.integers(0, 16, (N, DM, 8, L)); d = rng.integers(0, DM + 1, (N, L))
    return refs, gloss, f(rng, N, 128, W), f(rng, N, 128, L), need, v, p, a, d
def pack(refs, gloss, facts, cases, need, v, p, a, d):
    i = lambda x: np.ascontiguousarray(x).astype(np.int32)
    return {"refs": i(refs.reshape(N, 128, V)), "gloss": i(gloss.reshape(N, 128, W)), "facts": np.ascontiguousarray(facts).astype(BF), "cases": np.ascontiguousarray(cases).astype(BF), "need": i(need),
            "vp0": i(np.concatenate([v, p.reshape(N, 8 * DM, L)], axis=1)), "act0": i(a.reshape(N, 8 * DM, L)), "dep0": i(d.reshape(N, 1, L))}
def setup_inputs(rng):
    return pack(*parts(rng))
def skew(rng, n):
    e = rng.choice(np.array([1.0, 2.0, 4.0]), (N, 8, 16, 1)); x = np.minimum((W * rng.random((N, 8, 16, n)) ** e).astype(np.int64), W - 1)
    return np.where(rng.random((N, 8, 1, 1)) < 0.5, W - 1 - x, x)
def setup_inputs_spread(rng):
    refs, gloss, facts, cases, need, v, p, a, d = parts(rng)
    need = np.where(rng.random(need.shape) < 0.3, rng.integers(1, 129, need.shape), need)
    far = np.exp2(40.0 * (rng.permutation(128)[None, :, None] % 3 - 1)).astype(np.float32)
    return pack(skew(rng, V), skew(rng, W), wide(rng, N, 128, W).astype(np.float32) * far, wide(rng, N, 128, L).astype(np.float32) * far, need, v, p, a, d)
def tips(rng, x, top, share):
    return np.where(rng.random(x.shape) < share, top * rng.integers(0, 2, x.shape), x)
def setup_inputs_ends(rng):
    refs, gloss, facts, cases, need, v, p, a, d = parts(rng)
    al = rng.random((N, 1, L)) < 0.5; al[:, :, 0] = True; al[:, :, L - 1] = True
    bit = np.where(rng.random((N, 1, 16, V)) < 0.7, rng.integers(0, 2, (N, 1, 16, V)), rng.integers(0, 2, (N, 8, 16, V)))
    refs = np.where(rng.random(refs.shape) < 0.9, (W - 1) * bit, refs)
    refs[..., 0] = (W - 1) * (np.arange(16) & 1); refs[..., V - 1] = (W - 1) * (np.arange(16) == 15)
    gloss = tips(rng, gloss, W - 1, 0.85)
    for c in (0, W - 1): gloss[..., c] = (W - 1) * rng.integers(0, 2, (N, 8, 16))
    gloss[:, :, 0, 0] = 0; gloss[:, :, 0, W - 1] = W - 1; gloss[:, :, 15, 0] = W - 1; gloss[:, :, 15, W - 1] = 0
    v = (V - 1) * np.where(al, rng.integers(0, 2, (N, 1, L)), rng.integers(0, 2, (N, 8, L)))
    p = tips(rng, p, V - 1, 0.9); a = np.where(al[:, None], 15 * rng.integers(0, 2, (N, DM, 1, L)), tips(rng, a, 15, 0.9))
    d = tips(rng, d, DM, 0.8); d[:, 0] = DM; d[:, L - 1] = DM
    need = np.where(rng.random(need.shape) < 0.8, np.where(rng.random(need.shape) < 0.5, 1, 128), rng.integers(40, 90, need.shape))
    need[:, 0, 0] = 128; need[:, 0, L - 1] = 128
    facts[:, :, 0] = -64; facts[:, :, W - 1] = 64
    u = rng.random((N, 1, L)); u[:, :, 0] = 0.1; u[:, :, L - 1] = 0.1
    z = np.where(u < 0.25, np.float32(-64), cases.astype(np.float32)); one = rng.integers(0, 128, (N, 1, L)) == np.arange(128)[None, :, None]
    z = np.where(one & (u > 0.6) & (u < 0.8), np.float32(-128), np.where(one & (u >= 0.8), np.float32(128), z))
    return pack(refs, gloss, facts, z, need, v, p, a, d)
def setup_inputs_corners(rng):
    refs, gloss, facts, cases, need, v, p, a, d = parts(rng)
    facts = rng.integers(-3, 4, (N, 128, W)).astype(np.float32); z = rng.integers(-3, 4, (N, 128, L)).astype(np.float32)
    k = rng.integers(0, 6, (N, L)); k[:, :6] = np.arange(6); k[:, L - 6:] = np.arange(6)[::-1]
    cnt = np.where(k == 0, 128, np.where(k == 1, 0, np.where(k == 2, 64, rng.choice(np.array([1, 127]), (N, L)))))
    order = np.argsort(rng.random((N, 128, L)), axis=1)
    z = np.where((k < 4)[:, None, :], np.where(order < cnt[:, None, :], 1024.0, -1024.0), z)
    other = (np.arange(128)[None, :, None] >> 4) != rng.integers(0, 8, (N, 1, L))
    z = np.where((k == 5)[:, None, :] & other, 1024.0, z)
    kk = k[:, None, :]; s = need.shape
    need = np.where(kk < 2, np.where(rng.random(s) < 0.5, 1, 128), np.where(kk < 4, cnt[:, None, :] + rng.integers(0, 2, s), np.where(kk == 4, rng.integers(62, 84, s), rng.integers(118, 125, s))))
    ve = np.array([0, 1, V - 2, V - 1])
    v = np.where(rng.random(v.shape) < 0.7, rng.choice(ve, v.shape), v); p = np.where(rng.random(p.shape) < 0.7, rng.choice(ve, p.shape), p)
    a = np.where(rng.random(a.shape) < 0.7, rng.choice(np.array([0, 1, 14, 15]), a.shape), a)
    return pack(refs, gloss, facts, z, need, v, p, a, d)
def setup_inputs_crowd(rng):
    refs, gloss, facts, cases, need, v, p, a, d = parts(rng)
    a = rng.integers(8, 16, a.shape); a[:, 0] = rng.integers(1, 8, (N, 8, L))
    cases[:, :48] = 2048; cases[:, 48:96] = -2048; cases[:, 96:100] = 512
    for g in range(8):
        s = 1 + rng.permutation(W - 2)[:4]
        if g < 4:
            if g < 2: s[1] = (W - 1) * (1 - g)
            gloss[:, g, 8:, s[0]] = s[1]; gloss[:, g, 8:, s[1]] = s[1]; refs[:, g, 0] = s[0]
            if g >= 2:
                gloss[:, g, 8:, s[2]] = s[3]; gloss[:, g, 8:, s[3]] = s[3]
                w = int(rng.integers(0, V)); refs[:, g, 0, w] = s[2]
                v[:, g] = np.where(v[:, g] == w, (w + 1) % V, v[:, g]); v[np.arange(N), g, rng.integers(0, L, N)] = w
        elif g == 4:
            for c in s: gloss[:, g, 8:, c] = c
            refs[:, g] = s[rng.integers(0, 4, (N, 16, V))]
        elif g == 5:
            o = rng.permutation(W); own = o[:N * L]; rest = o[N * L:]; gg = gloss[:, g]
            gg[:, 8:, own] = own; gg[:, 8:, rest] = rest[rng.integers(0, W - N * L, (N, 8, W - N * L))]
            gg[:, 1:8, own] = 2 * (gg[:, 1:8, own] // 2); gg[:, 1:8, rest] = 2 * (gg[:, 1:8, rest] // 2) + 1
            refs[:, g, 0] = own.reshape(N, L)[:, np.arange(V) % L]; refs[:, g, 1:] = rest[rng.integers(0, W - N * L, (N, 15, V))]
            v[:, g] = np.argsort(rng.random((N, L)), axis=1) + L * rng.integers(0, V // L, (N, L))
            a[:, 0, g] = np.minimum(a[:, 0, g], 6); a[:, 0, g, L - 1] = 7
        else:
            gloss[:, g, 1:, s[0]] = s[0]; refs[:, g, 0] = s[0]; facts[:, 16 * g:16 * g + 16, s[0]] = 1024
    need = rng.integers(50, 58, need.shape); need[:, 0] = rng.integers(49, 53, (N, L)); need[::2, 2] = 128
    need[:, ST - 1] = np.where(rng.random((N, L)) < 0.5, 1, need[:, ST - 1])
    d[:] = DM; d[1::2] = np.where(rng.random(d[1::2].shape) < 0.1, rng.integers(0, DM, d[1::2].shape), DM)
    return pack(refs, gloss, facts, cases, need, v, p, a, d)
def setup_inputs_calm(rng):
    refs, gloss, facts, cases, need, v, p, a, d = parts(rng)
    hi = np.arange(8)[:, None] >= 4; few = np.where(hi, W - 4 + np.arange(4), np.arange(4))
    refs[:, :7] = hotty(rng, few, V, 1.0)[:, :7]; gloss[:, :7] = hotty(rng, few, W, 1.0)[:, :7]
    v = rng.integers(0, 4, v.shape) + (V - 4) * hi; p = rng.integers(0, 4, p.shape) + (V - 4) * hi; a = rng.integers(0, 4, a.shape) + 12 * hi
    return pack(refs, gloss, facts, cases, need, v, p, a, d)
def check_inputs(d):
    bad = []
    for k, lo, hi in (("refs", 0, W - 1), ("gloss", 0, W - 1), ("need", 1, 128), ("vp0", 0, V - 1), ("act0", 0, 15), ("dep0", 0, DM)):
        if np.min(d[k]) < lo or np.max(d[k]) > hi: bad.append("range of " + k)
    for k in ("facts", "cases"):
        if not np.all(np.isfinite(np.asarray(d[k]).astype(np.float32))): bad.append("not finite: " + k)
    return bad
def reference(refs, gloss, facts, cases, need, vp0, act0, dep0):
    R = refs.astype(np.int64).reshape(N, 8, 16, V); GL = gloss.astype(np.int64).reshape(N, 8, 16, W)
    X = facts.astype(np.float32).reshape(N, 8, 16, W); Z = cases.astype(np.float32).reshape(N, 8, 16, L)
    v = vp0[:, :8].astype(np.int64); p = vp0[:, 8:].astype(np.int64).reshape(N, DM, 8, L)
    a = act0.astype(np.int64).reshape(N, DM, 8, L); d = dep0[:, 0].astype(np.int64); c = need.astype(np.int64)
    gi = np.arange(8)[:, None, None]; lane = np.arange(L); shown = np.zeros((N, 8, 16, L), np.int64)
    for t in range(ST):
        writes = []
        for r in range(N):
            q = (r + 1 + t % (N - 1)) % N
            B = np.take_along_axis(R[r], v[r][:, None, :], 2)
            for j in range(DM, 1, -1): B = GL[r][gi, a[r, j - 1][:, None, :], B]
            a1 = np.array(a[r, 0]); T = GL[q][gi, a1[:, None, :], B]; shown[r] = T
            n = np.zeros((16, L), np.int64)
            for g in range(8): n = n + np.sum((X[q, g][:, T[g]] <= Z[r, g][:, None, :]).astype(np.int64), axis=0)
            met = n >= c[r, t][None, :]
            every = np.all(met, axis=0); some = np.any(met, axis=0); fu = np.argmin(met, axis=0); hm = np.argmax(met, axis=0)
            tf = T[:, fu, lane]; bf = B[:, fu, lane]; th = T[:, hm, lane]
            pop = every & (d[r] > 0); push = ~every & (d[r] < DM); put = ~every & some & (d[r] == DM)
            after = (v[r] + 1) & (V - 1); nv = np.where(push, tf & (V - 1), after)
            for j in range(1, DM + 1):
                leave = pop & (d[r] == j); enter = push & (d[r] == j - 1)
                nv = np.where(leave, p[r, j - 1], nv)
                a[r, j - 1] = np.where(enter, tf & 15, np.where(leave, 0, a[r, j - 1])); p[r, j - 1] = np.where(enter, after, p[r, j - 1])
            v[r] = nv; d[r] = d[r] + push.astype(np.int64) - pop.astype(np.int64)
            writes.append((q, a1, bf, th, np.nonzero(put)[0]))
        for q, a1, bf, th, who in writes:
            for g in range(8):
                places, first = np.unique(bf[g, who], return_index=True); w = who[first]
                GL[q, g, a1[g, w], bf[g, w]] = th[g, w]
    yvp = np.concatenate([v, p.reshape(N, 8 * DM, L)], axis=1)
    return {"yt": shown.reshape(N, 128, L).astype(np.float32), "yg": np.sum(GL.reshape(N, 128, 16, W // 16), axis=2).astype(np.float32), "yvp": yvp.astype(np.float32),
            "yact": a.reshape(N, 8 * DM, L).astype(np.float32), "ydep": d.reshape(N, 1, L).astype(np.float32)}

@@ -1,0 +1,694 @@
+import numpy as np
+from concourse.bass import DstId, RemoteDMATransfer
+from concourse.mybir import dt, AluOpType, AxisListType, ActivationFunctionType
+
+ALU = AluOpType
+ACT = ActivationFunctionType
+ST, NC = 6, 6
+TABW = 32768 + 256
+MW = 256 + 8 * NC
+BF, F32, I32, U16, F16 = "bfloat16", "float32", "int32", "uint16", "float16"
+
+SB = {
+    "tab": (TABW, BF), "gl": (2048, I32), "ghi": (2048, BF), "glo": (2048, BF), "fac": (2048, BF), "zer": (1024, BF),
+    "refw": (264, I32), "cn": (512, BF), "cl": (3 * 512, BF), "cr": (3 * 4096, BF), "nd": (256, I32), "dr": (256, BF),
+    "sin": (128, I32), "sinf": (128, F32), "trn": (128, F32),
+    "pi": (4, I32), "pf": (20, F32), "xcol": (256, F32), "xg": (128, F32), "sel": (144, BF), "go": (144, F16), "one": (144, BF),
+    "goa": (128, F16), "idb": (128, BF), "idh": (128, F16), "tri": (128, BF), "tri2": (128, BF), "tmpc": (128, F32),
+    "m2k": (128, BF), "pick": (768, BF), "pk0": (768, BF), "wa": (64, BF), "w2": (64, BF), "wf": (512, F32), "cc": (48, F16), "ccf": (48, F32),
+    "zc": (272, F16), "dum": (16, F32), "acc": (16, F32), "jh": (144, F32), "sl": (2, U16),
+    "st": (144, F32), "lu": (144, U16), "dh": (48, F32), "g1": (48, F32), "aft": (64, F32),
+    "p3": (64, I32), "we": (48, F32), "wn": (96, I32), "wt": (48, F32), "wl": (48, F32), "wu": (96, F32), "wy": (48, F32),
+    "wm": (48, F32), "wx": (96, F32), "ww": (48, F32), "nb2": (16, F32), "sa": (16, F32), "sc": (16, F32), "jk": (32 * 272, BF), "wen": (48, F32), "w01": (32, F32), "wd": (16, F32),
+    "ra": (768, BF), "o3f": (256, F32), "o3": (256, U16), "o2": (256, U16), "of": (256, U16),
+    "g3": (4096, BF), "g2": (4096, BF), "gt": (4096, BF), "cm": (4096, BF),
+    "sb": (ST * MW, U16), "lb": (ST * MW, U16), "ps": (ST * 16, I32), "pl": (ST * 16, I32),
+    "o32": (256, F32), "bk": (256, F16), "ac": (16, F32), "ac2": (16, F32), "uu": (256, BF), "ohf": (256, BF), "ohk": (256, F16),
+    "xx": (768, F16), "hl": (16, U16), "nb": (16, F32), "kb": (16, F32), "ab": (8 * 272, F32), "nm": (16, F32),
+    "wo": (16, U16), "th": (256, BF), "tl": (256, U16), "tf": (256, F32), "fo": (2 * 1152, F32), "ygs": (128, F32),
+}
+SCRATCH = {k: ("sbuf", [128, v[0]], v[1]) for k, v in SB.items()}
+for _b in range(8):
+    SCRATCH["pb%d" % _b] = ("psum", [128, 512], F32)
+SEMAPHORES = (["sv", "ss", "sp", "sg", "loc", "yta"] + ["c%d" % i for i in range(3)] + ["b%d" % i for i in range(ST * NC)]
+              + ["p%d" % i for i in range(ST * NC)] + ["d%d" % i for i in range(24)])
+ESEM = {"V": "sv", "S": "ss", "P": "sp", "G": "sg"}
+GA, SCA, PEC = 1.56, 3.8, 0.5
+LAT_X, LAT_S, LAT_R, LAT_D = 120.0, 70.0, 2600.0, 2000.0
+PRM = {"ch":[0,64,128,192,256],"split":{"00":2,"01":2,"02":2,"03":2,"10":2,"11":2,"12":2,"13":2,"20":2,"21":2,"22":2,"23":2,"30":2,"31":2,"32":2,"33":2},
+       "off":{"yvp:e1":-47,"cn:s":24,"ygs":-150,"yact:e1":-77,"1x":-83,"gt":77,"yvp":13,"wn":-3,"zer:s":-20,"ra:b1y":90,"zc:s":-9,"wx":0,"yact:e0":80,"yvp:e0":27,"wy":110,"yg":3,"xg:s":-4,"yact":30,"of":-160,"o2":-77,"ps":-10,"xcol:s":10,"ww":-10,"1b":-80},
+       "eng":{"ra:b0":"V","ra:b1":"S","ra:b0y":"S","ra:b1y":"S","ohf:2":"V","fo:e0":"S","nb:3":"S","nb:2":"S","dh:s":"S","fo:e1":"V","th:3":"S","nm:2":"V","nb:0":"S","ohf:0":"V","ygs:e1":"V","nb2:2":"S","nb2:0":"S"},
+       "win":50.0,"both":0,"dfill":3,"small":3000,"uv":[3],
+       "seq":{"V":["g3:0a","g2:0b","g3:2b","g2:1b","g3:3b","g2:2a","g2:3a","gt:0a","cm:0b","cm:0a","cm:1a","cm:1b","cm:2b","cm:2a","cm:3a","cm:3b"],
+              "S":["g3:0b","g3:1b","g3:1a","g2:0a","g3:2a","g2:1a","g3:3a","g2:2b","gt:0b","g2:3b","gt:1a","gt:1b","gt:2a","gt:2b","gt:3a","gt:3b"]},"rounds":4}
+
+
+def A(n, c0, c1, cs=1, p0=0, p1=128, ps=1):
+    return (n, (p0, p1, ps), (c0, c1, cs))
+
+
+def IND(win, off):
+    return ("ind", win, off)
+
+
+def isap(x):
+    return isinstance(x, tuple)
+
+
+def ncol(a):
+    if a[0] == "ind":
+        return 16 * ncol(a[2])
+    return len(range(*a[2]))
+
+
+def meet(r, s):
+    if r[1] <= s[0] or s[1] <= r[0]:
+        return False
+    return not (r[2] == s[2] and r[2] > 1 and (r[0] - s[0]) % r[2])
+
+
+def real(T, a):
+    if not isap(a):
+        return a
+    if a[0] == "ind":
+        return real(T, a[1]).indirect(real(T, a[2]))
+    p, c = a[1], a[2]
+    return T[a[0]][slice(p[0], p[1], p[2]) if p[2] > 1 else slice(p[0], p[1]), slice(c[0], c[1], c[2]) if c[2] > 1 else slice(c[0], c[1])]
+
+
+def program(prm):
+    ops, hist, nd, tag = [], {}, [0], ["s"]
+    CH, split = prm["ch"], prm["split"]; NC = len(CH) - 1
+    both = list(range(NC - prm["both"], NC))
+    PO = [sum(CH[j + 1] - CH[j] for j in range(c % 2, c, 2)) for c in range(NC)]
+    def msg(t, c):
+        return t * MW + CH[c] + 8 * c
+
+    def add(alts, outs, ins, kind="c", lat=0.0, extra=None, after=()):
+        rd, wr = [], []
+        for a in ins:
+            if isap(a):
+                rd += [a[1], a[2]] if a[0] == "ind" else [a]
+        for a in outs:
+            if a[0] == "ind":
+                wr.append(a[1]); rd.append(a[2])
+            else:
+                wr.append(a)
+        me = len(ops); deps = set(after); raw = set(after)
+        for lst, w in ((rd, False), (wr, True)):
+            for a in lst:
+                for (b, o, bw) in hist.get(a[0], ()):
+                    if (w or bw) and meet(a[1], b[1]) and meet(a[2], b[2]):
+                        deps.add(o); raw.add(o)
+        for lst, w in ((rd, False), (wr, True)):
+            for a in lst:
+                h = hist.setdefault(a[0], [])
+                if w:
+                    h[:] = [e for e in h if e[0] != a]
+                h.append((a, me, w))
+        banks = sorted(set(a[0] for a in rd + wr if a[0][:2] == "pb"))
+        ops.append({"alts": alts, "deps": deps, "raw": raw, "banks": banks, "kind": kind, "lat": lat, "x": extra,
+                    "n": "%s:%s" % ((wr or rd)[0][0], tag[0])})
+        return me
+
+    def two(*aps):
+        return all(a[0] in SB and SB[a[0]][1] in (BF, F16, U16) for a in aps)
+
+    def vcost(out, in0, in1=None):
+        if out[0] == "ind":
+            return 60 + SCA * ncol(out)
+        n = ncol(out)
+        if in0[0] == "ind":
+            return 60 + GA * n
+        c = 2.0 if (in1 is not None and in0[0][:2] != "pb" and in1[0][:2] != "pb") else 1.0
+        if two(out, in0) and (in1 is None or two(in1)):
+            c *= 0.5
+        return max(64.0, c * n)
+
+    def scost(out, in0):
+        return 75 + GA * ncol(out) if in0[0] == "ind" else max(64.0, 30 + ncol(out))
+
+    def e_act(out, in_, f, bias=None, scale=None):
+        kw = {}
+        def em(g, T):
+            k = {}
+            if bias is not None: k["bias"] = real(T, bias)
+            if scale is not None: k["scale"] = real(T, scale)
+            return g.scalar.activation(real(T, out), real(T, in_), f, **k)
+        return em
+
+    def e_ts(out, in0, s1, s2, op0, op1):
+        if op1 is None:
+            return lambda g, T: g.vector.tensor_scalar(real(T, out), real(T, in0), real(T, s1), None, op0)
+        return lambda g, T: g.vector.tensor_scalar(real(T, out), real(T, in0), real(T, s1), real(T, s2), op0, op1)
+
+    def cp(out, in_, eng="V"):
+        alts = {}
+        if "V" in eng: alts["V"] = (vcost(out, in_), lambda g, T: g.vector.tensor_copy(real(T, out), real(T, in_)))
+        if "S" in eng: alts["S"] = (scost(out, in_), e_act(out, in_, ACT.Copy))
+        return add(alts, [out], [in_])
+
+    def tt(out, a, b, op):
+        return add({"V": (vcost(out, a, b), lambda g, T: g.vector.tensor_tensor(real(T, out), real(T, a), real(T, b), op))}, [out], [a, b])
+
+    def ts(out, in0, s1, s2, op0, op1=None, salt=None):
+        alts = {"V": (vcost(out, in0), e_ts(out, in0, s1, s2, op0, op1))}
+        ins = [in0, s1, s2]
+        if salt is not None:
+            alts["S"] = (scost(out, in0), e_act(out, in0, *salt)); ins += list(salt[1:])
+        return add(alts, [out], ins)
+
+    def act(out, in_, f, bias=None, scale=None):
+        return add({"S": (scost(out, in_), e_act(out, in_, f, bias, scale))}, [out], [in_, bias, scale])
+
+    def ms(out, val):
+        return add({"V": (max(64.0, ncol(out) * (0.5 if two(out) else 1.0)), lambda g, T: g.vector.memset(real(T, out), val))}, [out], [])
+
+    def io(out, pat, base, cm):
+        fl = SB[out[0]][1] != I32
+        def em(g, T):
+            if fl: return g.iota(real(T, out), pat, base, cm, allow_small_or_imprecise_dtypes=True)
+            return g.iota(real(T, out), pat, base, cm)
+        return add({"G": (150 + 2.0 * ncol(out), em)}, [out], [])
+
+    def mm(lst):
+        def em(g, T):
+            r = None
+            for (o, l, rh, s0, s1) in lst:
+                r = g.tensor.matmul(real(T, o), real(T, l), real(T, rh), s0, s1)
+            return r
+        return add({"P": (60 + sum(PEC * max(64, ncol(m[2])) for m in lst), em)}, [m[0] for m in lst], [m[1] for m in lst] + [m[2] for m in lst])
+
+    def dma(pairs, q, nbytes):
+        sem = "d%d" % nd[0]; nd[0] += 1
+        def em(g, T):
+            for (o, i) in pairs:
+                (g.sync if q == "Y" else g.scalar).dma_start(real(T, o), real(T, i)).then_inc(T.sem[sem], 16)
+        return add({q: (100.0 * len(pairs), em)}, [p[0] for p in pairs], [p[1] for p in pairs], "d", nbytes / 250.0, (sem, 16 * len(pairs)))
+
+    def send(src, dst, sem, step, back, arrive=True, after=(), n=1):
+        s = add({"G": (150.0, None)}, [], [src], "r", 0.0, (src, dst, sem, step, back))
+        if arrive is True:
+            return add({}, [dst], [], "a", LAT_R + 128 * ncol(src) * 2 / 50.0, (sem, 8), after=[s])
+        if arrive:
+            return add({}, [arrive], [], "a", LAT_R, (sem, 8 * n), after=[s] + list(after))
+        return s
+
+    def D(n, r0, r1, c0, c1, rs=1):
+        return A(n, c0, c1, 1, r0, r1, rs)
+
+    def col(n, c):
+        return A(n, c, c + 1)
+
+    for h in range(2):
+        dma([(A("gl", 1024 * h, 1024 * h + 1024), D("gloss", 0, 128, 1024 * h, 1024 * h + 1024))], "Y", 1 << 19)
+    ms(A("sin", 0, 128), 0)
+    ms(A("zer", 0, 1024), 0.0)
+    dma([(A("cn", 0, 256), D("cases", 0, 128, 0, 256)), (A("nd", 0, 256, 1, 0, 6), D("need", 0, 6, 0, 256)),
+         (A("nd", 0, 256, 1, 32, 33), D("dep0", 0, 1, 0, 256))], "Y", 70000)
+    prs = []
+    for q in range(7):
+        for g1 in range(2):
+            src = D("vp0", 8 * q + g1, 8 * q + 8, 0, 256, 2) if q < 4 else D("act0", 8 * (q - 4) + g1, 8 * (q - 4) + 8, 0, 256, 2)
+            c0 = (q // 2) * 32 + g1 * 16
+            prs.append((A("sin", c0, c0 + 16, 1, q % 2, 128, 2), src))
+    dma(prs, "Y", 30000)
+    dma([(A("refw", 0, 256), D("refs", 0, 128, 0, 256)), (A("refw", 256, 264), D("refs", 0, 128, 0, 8))], "Y", 1 << 17)
+    dma([(A("fac", 0, 2048), D("facts", 0, 128, 0, 2048))], "Y", 1 << 19)
+    io(col("pi", 0), [[0, 1]], 0, 1)
+    io(A("xcol", 0, 256), [[1, 256]], 0, 0)
+    io(A("xg", 0, 128), [[16, 8], [0, 16]], 0, 0)
+    io(A("wa", 0, 64), [[0, 4], [2048, 16]], 0, 0)
+    ts(col("pi", 1), col("pi", 0), 112, None, ALU.bitwise_and)
+    ts(col("pi", 2), col("pi", 0), 15, None, ALU.bitwise_and)
+    ts(col("pi", 3), col("pi", 0), 7, None, ALU.bitwise_and)
+    cp(A("pf", 0, 2), A("pi", 1, 3)); cp(col("pf", 8), col("pi", 0))
+    cp(col("sl", 0), col("pi", 3)); cp(col("sl", 1), col("pi", 3))
+    k = col("pf", 1)
+    ts(col("pf", 2), col("pf", 0), 15.0, None, ALU.add)
+    ts(col("pf", 3), k, 2.0, None, ALU.is_lt)
+    ts(col("pf", 4), k, 16.0, None, ALU.add)
+    ts(col("pf", 5), k, -0.5, -7.0, ALU.mult, ALU.add)
+    ts(col("pf", 9), k, 0.0, 2.0, ALU.is_equal, ALU.mult)
+    tt(col("pf", 6), col("pf", 9), col("pf", 4), ALU.add)
+    ts(col("pf", 7), col("pf", 4), -1.0, None, ALU.mult)
+    ts(A("pf", 16, 20), A("pf", 4, 8), 0.5, None, ALU.mult)
+    ts(A("sel", 0, 144), A("xcol", 0, 144), col("pf", 2), col("pf", 3), ALU.is_equal, ALU.mult)
+    ts(A("idb", 0, 128), A("xcol", 0, 128), col("pf", 8), None, ALU.is_equal)
+    ms(A("one", 0, 144), 0.0); ms(A("one", 15, 144, 16), 1.0)
+    ms(A("m2k", 0, 128), -2048.0)
+    for h in range(2):
+        c = (1024 * h, 1024 * h + 1024)
+        cp(A("ghi", *c), A("gl", *c))
+    for h in range(2):
+        c = (1024 * h, 1024 * h + 1024)
+        tt(A("glo", *c), A("gl", *c), A("ghi", *c), ALU.subtract)
+    tag[0] = "sd"
+    for i in range(prm["dfill"]):
+        dma([(A("tab", TABW - 2048 * (i + 1), TABW - 2048 * i), D("facts", 0, 128, 0, 2048))], "Y", 1 << 19)
+    tag[0] = "s"
+    for c0 in range(0, TABW - 2048 * prm["dfill"], 1024):
+        o = A("tab", c0, min(TABW - 2048 * prm["dfill"], c0 + 1024)); n = ncol(o)
+        def gfill(g, T, o=o, n=n):
+            return g.iota(real(T, o), [[0, n]], 0, 0, allow_small_or_imprecise_dtypes=True)
+        add({"V": (0.5 * n, lambda g, T, o=o: g.vector.memset(real(T, o), 0.0)), "S": (30 + n, e_act(o, A("zer", 0, n), ACT.Copy)),
+             "G": (150 + 2.0 * n, gfill)}, [o], [A("zer", 0, n)])
+    dma([(A("tab", 0, 32768, 1, 0, 128, 16), A("ghi", 0, 2048))], "Y", 1 << 19)
+    dma([(A("tab", 0, 32768, 1, 1, 128, 16), A("glo", 0, 2048))], "S", 1 << 19)
+    ms(A("cn", 256, 512), 0.0)
+    cp(A("cn", 256, 512, 1, 0, 6), A("nd", 0, 256, 1, 0, 6))
+    cp(A("dr", 0, 256, 1, 32, 33), A("nd", 0, 256, 1, 32, 33))
+    for s in range(3):
+        send(A("cn", 0, 512), A("cl", 512 * s, 512 * s + 512), "c%d" % s, s, False)
+    cp(A("sinf", 0, 128), A("sin", 0, 128), "V")
+    add({"V": (128.0, lambda g, T: g.vector.transpose(T.trn[:], T.sinf[:]))}, [A("trn", 0, 128)], [A("sinf", 0, 128)])
+    mm([(A("pb6", 0, 16), A("one", 15 - lo, 143 - lo, 1, 32, 33), A("dr", lo, 256, 16, 32, 33), lo == 0, lo == 15) for lo in range(16)])
+    def S_(b, s, n=1, buf="st"):
+        return A(buf, 72 * b + 8 * s, 72 * b + 8 * (s + n))
+    def W(n, b, j0=0, j1=3):
+        return A(n, 24 * b + 8 * j0, 24 * b + 8 * j1)
+    io(A("jh", 0, 144), [[1, 6], [-1, 3], [0, 8]], 3, 0)
+    for b in range(2):
+        for q, s in ((0, 0), (6, 1), (5, 2), (4, 3), (3, 4), (2, 5), (1, 6)):
+            c0 = (q // 2) * 32 + q % 2 + 16 * b
+            cp(S_(b, s), A("trn", c0, c0 + 15, 2), "VS")
+        for j in range(3):
+            cp(W("dh", b, j, j + 1), A("pb6", 8 * b, 8 * b + 8), "VS")
+    io(A("w2", 0, 64), [[1024, 4], [-2048, 16]], -2048, 0)
+    ts(A("go", 0, 144), A("xcol", 0, 144), col("pf", 2), None, ALU.is_equal)
+    ts(A("goa", 0, 128), A("xg", 0, 128), col("pf", 0), None, ALU.is_equal)
+    ts(A("idh", 0, 128), A("xcol", 0, 128), col("pf", 8), None, ALU.is_equal)
+    ts(A("tmpc", 0, 128), A("xcol", 0, 128), col("pf", 8), -1.0, ALU.is_gt, ALU.mult)
+    tt(A("tmpc", 0, 128), A("tmpc", 0, 128), A("goa", 0, 128), ALU.mult)
+    ts(A("tri2", 0, 128), A("idb", 0, 128), 16.0, None, ALU.mult)
+    tt(A("tri", 0, 128), A("tri2", 0, 128), A("tmpc", 0, 128), ALU.add)
+    cp(A("tri2", 0, 128), A("tri", 0, 128))
+    ts(A("tmpc", 0, 8), A("idb", 0, 128, 16), 32.0, None, ALU.mult)
+    tt(A("tri2", 0, 128, 16), A("tmpc", 0, 8), A("goa", 0, 128, 16), ALU.subtract)
+    pk0, pk = A("pk0", 0, 768, 1, 0, 32), A("pick", 0, 768, 1, 0, 32)
+    ms(pk0, -1.0)
+    add({"G": (1700.0, lambda g, T: g.affine_select(real(T, pk), real(T, pk0), [[1, 6], [0, 128]], ALU.is_equal, 0.0, 0, -1))}, [pk], [pk0])
+    ts(col("pf", 10), k, 16.0, None, ALU.mult)
+    ts(col("pf", 11), k, -1.0 / 1024, None, ALU.mult)
+    ms(A("ccf", 0, 48), 0.0)
+    for c in range(NC):
+        h0, h1 = CH[c] // 16, CH[c + 1] // 16; nh = h1 - h0
+        ts(A("ccf", 3 * h0 + nh, 3 * h0 + 2 * nh), A("xcol", h0, h1), 1.0 / (64 if c in both else 32), None, ALU.mult)
+        ts(A("ccf", 3 * h0 + 2 * nh, 3 * h0 + 3 * nh), A("xcol", h0, h1), 256.0, col("pf", 10), ALU.mult, ALU.add)
+    cp(A("cc", 0, 48), A("ccf", 0, 48))
+    ts(A("zc", 0, 16), A("xcol", 0, 16), 0.0, col("pf", 11), ALU.mult, ALU.add)
+    ts(col("pf", 12), col("pf", 11), 1.0 / 512, None, ALU.add)
+    ts(A("zc", 16, 272), A("xcol", 0, 256), 1.0 / 512, col("pf", 12), ALU.mult, ALU.add)
+    ts(col("pf", 13), k, 32768.0, None, ALU.add)
+    ts(A("dum", 0, 16), A("xcol", 0, 16), 16.0, col("pf", 13), ALU.mult, ALU.add)
+    ts(A("acc", 0, 16), A("dum", 0, 16), -32766.0, 32768.0, ALU.add, ALU.mult)
+    ts(col("pf", 14), k, 1.0 / 1024, 31.0 / 64, ALU.mult, ALU.add)
+    ts(col("pf", 15), col("pf", 11), -1.0 / 1024, None, ALU.add)
+    io(A("wf", 0, 512), [[0, 2], [1, 256]], 0, 0)
+
+    tabw = A("tab", 0, TABW)
+
+    def update(t, b):
+        p = A("p3", 32 * b, 32 * b + 24); q = 48 * b
+        na, tv, nt = A("wn", q, q + 24), A("wn", q + 24, q + 48), A("wn", q, q + 48)
+        da, x, dx = A("wx", q, q + 24), A("wx", q + 24, q + 48), A("wx", q, q + 48)
+        ua, up, uu = A("wu", q, q + 24), A("wu", q + 24, q + 48), A("wu", q, q + 48)
+        cp(A("p3", 32 * b, 32 * b + 32), IND(A("pl", 16 * t + 8 * b, 16 * t + 8 * b + 8), A("sl", 0, 2)))
+        ts(W("we", b), p, 0.0, None, ALU.is_lt)
+        ts(tv, p, 255, None, ALU.bitwise_and)
+        ts(na, p, 15, None, ALU.bitwise_and)
+        tt(W("wl", b), W("we", b), W("dh", b), ALU.add)
+        tt(dx, nt, S_(b, 1, 6), ALU.subtract)
+        tt(W("wm", b), W("wl", b), A("jh", 24 * t, 24 * t + 24), ALU.is_equal)
+        tt(x, x, W("we", b), ALU.mult)
+        tt(W("wt", b), W("wl", b), W("we", b), ALU.add)
+        tt(W("wy", b), x, W("g1", b), ALU.subtract)
+        tt(ua, da, W("wm", b), ALU.mult)
+        tt(W("wen", b), W("wm", b), W("we", b), ALU.mult)
+        tt(W("ww", b), W("wy", b), W("wm", b), ALU.mult)
+        tt(up, W("wen", b), W("g1", b), ALU.mult)
+        w0, w1 = A("w01", 16 * b, 16 * b + 8), A("w01", 16 * b + 8, 16 * b + 16)
+        tt(w0, W("ww", b, 0, 1), W("ww", b, 1, 2), ALU.add)
+        tt(w1, W("ww", b, 2, 3), A("aft", 32 * b, 32 * b + 8), ALU.add)
+        tt(S_(b, 1, 6), S_(b, 1, 6), uu, ALU.add)
+        tt(S_(b, 0), w0, w1, ALU.add)
+        ts(W("dh", b), W("wt", b), t + 1.0, t + 4.0, ALU.max, ALU.min)
+
+    def lists(t, b):
+        cp(S_(b, 0, 4, "lu"), S_(b, 0, 4))
+        r = 384 * b
+        cp(A("ra", r, r + 128), IND(A("wa", 0, 64), S_(b, 1, 1, "lu")), "VS")
+        o = (128 * b, 128 * b + 128)
+        tt(A("o3f", *o), IND(A("refw", 0, 264), S_(b, 0, 1, "lu")), A("ra", r, r + 128), ALU.add)
+        cp(A("o3", *o), A("o3f", *o))
+        tag[0] += "y"
+        cp(A("ra", r + 128, r + 384), IND(A("wa", 0, 64), S_(b, 2, 2, "lu")), "VS")
+        wd = A("wd", 8 * b, 8 * b + 8)
+        ts(wd, W("dh", b, 0, 1), t + 3.0, 32.0, ALU.is_lt, ALU.mult)
+        tt(S_(b, 8), wd, S_(b, 3), ALU.add)
+        for c in range(NC):
+            if CH[c] // 128 == b:
+                w = CH[c + 1] - CH[c]; m = msg(t, c) + w; s0 = 72 * b + 64 + CH[c] % 128 // 16
+                cp(A("sb", m, m + w // 16), A("st", s0, s0 + w // 16))
+        ts(A("aft", 32 * b, 32 * b + 32), IND(S_(b, 0), A("sl", 0, 2)), 1.0, None, ALU.add)
+        tt(W("g1", b), A("aft", 32 * b, 32 * b + 24), S_(b, 4, 3), ALU.subtract)
+
+    def gather(buf, c, off, o0, stage):
+        n = split.get("%d%d" % (stage, c), 1); w = (CH[c + 1] - CH[c]) // n
+        for i in range(n):
+            tag[0] = "%d%s" % (c, "ab"[i] if n > 1 else "")
+            cp(A(buf, 16 * (CH[c] + w * i), 16 * (CH[c] + w * i + w)), IND(tabw, A(off, o0 + w * i, o0 + w * (i + 1))), "VS")
+        tag[0] = str(c)
+
+    def pick(out, buf, c, first):
+        mm([(out, A("idb", 0, 128), first, True, False)]
+           + [(out, A("sel", 15 - kk, 143 - kk), A(buf, 16 * CH[c] + kk, 16 * CH[c + 1], 16), False, kk == 15) for kk in range(16)])
+
+    yts = []
+    for t in range(ST):
+        s = t % 3
+        for b in range(2):
+            tag[0] = "b%d" % b
+            if t: update(t - 1, b)
+            lists(t, b)
+        tag[0] = "r%d" % t
+        if t < 3:
+            for kk in range(16):
+                cp(A("cr", 4096 * s + kk, 4096 * s + 4096, 16), A("cl", 512 * s, 512 * s + 256), "VS")
+        for c in range(NC):
+            l = (CH[c], CH[c + 1]); w = l[1] - l[0]; b = l[0] // 128; r = 384 * b + l[0] % 128; m = msg(t, c)
+            bank = "pb%d" % (c % 2); r0 = 2 * PO[c]
+            gather("g3", c, "o3", l[0], 3)
+            tag[0] = "%dx" % c
+            pick(A(bank, r0, r0 + w), "g3", c, A("ra", r + 128, r + 128 + w))
+            tag[0] = str(c)
+            cp(A("o2", *l), A(bank, r0, r0 + w))
+            gather("g2", c, "o2", l[0], 2)
+            pick(A(bank, r0 + w, r0 + 2 * w), "g2", c, A("ra", r + 256, r + 256 + w))
+            cp(A("sb", m, m + w), A(bank, r0 + w, r0 + 2 * w))
+            send(A("sb", m, m + w + w // 16), A("lb", m, m + w + w // 16), "b%d" % (t * NC + c), t, False)
+        for c in range(NC):
+            l = (CH[c], CH[c + 1]); w = l[1] - l[0]; m = msg(t, c); h = (l[0] // 16, l[1] // 16); nh = w // 16
+            pt = A("pb%d" % (2 + c % 2), PO[c], PO[c] + w)
+            vb = "pb%d" % (4 + c % 2); v0 = 3 * PO[c]
+            gather("gt", c, "lb", m, 1)
+            pick(pt, "gt", c, A("m2k", 0, w))
+            ts(A("of", *l), pt, 2048.0, None, ALU.add)
+            n = split.get("0%d" % c, 1)
+            for i in range(n):
+                tag[0] = "%d%s" % (c, "ab"[i] if n > 1 else ""); u = (l[0] + i * w // n, l[0] + (i + 1) * w // n)
+                tt(A("cm", 16 * u[0], 16 * u[1]), IND(A("fac", 0, 2048), A("of", *u)),
+                   A("cr", 4096 * s + 16 * u[0], 4096 * s + 16 * u[1]), ALU.is_le)
+            tag[0] = str(c)
+            if t == ST - 1:
+                last = c == NC - 1
+                yts.append(send(A("of", *l), A("tl", *l), "yta", t, True, A("tl", 0, 256) if last else False, yts, NC))
+            cp(A("o32", *l), A("lb", m, m + w))
+            tt(A("bk", *l), IND(A("w2", 0, 64), A("lb", m + w, m + w + nh)), A("o32", *l), ALU.add)
+            ts(A("ac", *h), A("lb", m + w, m + w + nh), 2048.0, 2048.0, ALU.mult, ALU.add)
+            if c in both:
+                tt(A("ac", *h), A("ac", *h), A("acc", *h), ALU.add)
+            cnt, ps, ps2 = A(vb, v0, v0 + w), A(vb, v0 + w, v0 + 2 * w), A(vb, v0 + 2 * w, v0 + 3 * w)
+            n0 = 512 * s + 256 + l[0]
+            tag[0] = "%dx" % c
+            mm([(cnt, A("pick", 128 * t, 128 * t + 128, 1, 0, 6), A("cl", n0, n0 + w, 1, 0, 6), True, False)]
+               + [(cnt, A("one", 15 - kk, 143 - kk), A("cm", 16 * l[0] + kk, 16 * l[1], 16), False, kk == 15) for kk in range(16)])
+            tag[0] = str(c)
+            uv = c in prm["uv"]; e0 = 12 if uv else 0
+            if uv: ts(A("uu", *l), cnt, 0.0, 0.5, ALU.is_lt, ALU.subtract)
+            else: act(A("uu", *l), cnt, ACT.Sign, -0.5, -1.0)
+            mm([(ps2, A("tri2", 0, 128), A("uu", *l), True, True), (ps, A("tri", 0, 128), A("uu", *l), True, True)])
+            x0 = 3 * l[0]
+            ts(A("ohf", *l), ps, col("pf", 4 + e0), None, ALU.is_ge, None, (ACT.Relu, col("pf", 5), 1.0 if uv else 0.5))
+            ts(A("ohk", *l), ps2, col("pf", 6 + e0), None, ALU.is_ge)
+            tt(A("xx", x0 + w, x0 + 2 * w), A("ohk", *l), A("bk", *l), ALU.mult)
+            tt(A("xx", x0, x0 + w), pt, A("ohf", *l), ALU.mult)
+            ts(A("xx", x0 + 2 * w, x0 + 3 * w), ps, col("pf", 7 + e0), k, ALU.is_le, ALU.mult)
+            z0 = 0 if c == 0 else 16 + l[0]; z1 = 16 + l[1]
+            mm([(A("pb7", z0, z1), A("idh", 0, 128), A("zc", z0, z1), True, False),
+                (A("pb7", z1 - w, z1), A("goa", 0, 128), A("xx", x0 + w, x0 + 2 * w), False, True)])
+            q0 = 3 * h[0]
+            pc = A("pb6", q0, q0 + 3 * nh)
+            mm([(pc, A("idh", 0, 128), A("cc", q0, q0 + 3 * nh), True, False)]
+               + [(pc, A("go", 15 - lo, 143 - lo), A("xx", x0 + lo, x0 + 3 * w, 16), False, lo == 15) for lo in range(16)])
+            key = A("pb6", q0 + nh, q0 + 2 * nh)
+            if c in both:
+                ts(A("nb", *h), key, -2.0 ** 25, None, ALU.mult, None, (ACT.Copy, None, -2.0 ** 25))
+            else:
+                ts(A("nb", *h), key, -1.0, col("pf", 14), ALU.mult, ALU.add, (ACT.Identity, col("pf", 14), -1.0))
+                ts(A("nb2", *h), key, -1.0, col("pf", 15), ALU.mult, ALU.add, (ACT.Identity, col("pf", 15), -1.0))
+            pp = (16 * t + h[0], 16 * t + h[1])
+            cp(A("ps", *pp), A("pb6", q0, q0 + nh))
+            if h[1] % 8 == 0:
+                pp = (pp[1] - 8, pp[1])
+                send(A("ps", *pp), A("pl", *pp), "p%d" % (t * NC + c), t, True)
+            cp(A("hl", *h), A("pb6", q0 + 2 * nh, q0 + 3 * nh))
+            tt(A("kb", *h), key, A("ac", *h), ALU.add)
+            for j in range(*h):
+                n = 17 + 16 * j; a0 = 272 * (j % 8); ab = A("ab", a0, a0 + n)
+                if c not in both:
+                    for bc, acc in ((col("nb", j), col("sa", j)), (col("nb2", j), col("sc", j))):
+                        z = A("pb7", 15, 15 + n); a0 = 272 * (2 * j + (acc[0] == "sa")); jk = A("jk", a0, a0 + n)
+                        add({"S": (50.0 + n, lambda g, T, z=z, jk=jk, bc=bc, acc=acc: g.scalar.activation(
+                            real(T, jk), real(T, z), ACT.Sign, bias=real(T, bc), accum_out=real(T, acc)))}, [acc, jk], [z, bc])
+                    continue
+                act(ab, A("pb7", 15, 15 + n), ACT.Abs, col("nb", j), 2.0 ** 25)
+                add({"V": (max(64.0, n), lambda g, T, ab=ab, j=j: g.vector.tensor_reduce(real(T, col("nm", j)), real(T, ab), AxisListType.X, ALU.min, negate=True))},
+                    [col("nm", j)], [ab])
+                if c == NC - 1:
+                    ts(col("wo", j), col("nm", j), col("kb", j), col("dum", j), ALU.add, ALU.min)
+            if c >= NC - 2:
+                u = (0, h[1]) if c == NC - 2 else h
+                cp(A("th", 16 * u[0], 16 * u[1]), IND(A("gt", 0, 16 * l[1]), A("hl", *u)), "VS")
+                js = [j for j in range(*u) if max(x for x in range(NC) if CH[x] <= 16 * j) not in both]
+                if js:
+                    v = (js[0], js[-1] + 1)
+                    tt(A("nm", *v), A("sa", *v), A("sc", *v), ALU.subtract)
+                    ts(A("nm", *v), A("nm", *v), 32768.0, None, ALU.mult, None, (ACT.Copy, None, 32768.0))
+                if c == NC - 2 or js:
+                    tt(A("nm", *u), A("nm", *u), A("kb", *u), ALU.add)
+                    tt(A("nm", *u), A("nm", *u), A("dum", *u), ALU.min)
+                    cp(A("wo", *u), A("nm", *u))
+        for c in (NC - 2, NC - 1):
+            tag[0] = str(c); u = (0 if c == NC - 2 else CH[c] // 16, CH[c + 1] // 16)
+            cp(IND(tabw, A("wo", *u)), A("th", 16 * u[0], 16 * u[1]))
+    tag[0] = "e"
+    dma([(A("ghi", 0, 2048), A("tab", 0, 32768, 1, 0, 128, 16))], "Y", 1 << 19)
+    dma([(A("glo", 0, 2048), A("tab", 0, 32768, 1, 1, 128, 16))], "S", 1 << 19)
+    cp(A("tf", 0, 256), A("tl", 0, 256))
+    dma([(D("yt", 0, 128, 0, 256), A("tf", 0, 256))], "Y", 1 << 17)
+    for b in range(2):
+        tag[0] = "e%d" % b
+        update(ST - 1, b)
+        ts(S_(b, 7), W("dh", b, 0, 1), -float(ST), None, ALU.add)
+        cp(S_(b, 0, 8, "lu"), S_(b, 0, 8))
+        f = 1024 * b
+        cp(A("fo", f, f + 512), IND(A("wf", 0, 512), S_(b, 0, 4, "lu")), "VS")
+        cp(A("fo", f + 512, f + 1024), IND(A("wf", 0, 512), S_(b, 4, 4, "lu")), "VS")
+        prs = []
+        for sl, name, r0 in ((0, "yvp", 0), (6, "yvp", 8), (5, "yvp", 16), (4, "yvp", 24), (3, "yact", 0), (2, "yact", 8), (1, "yact", 16)):
+            prs.append((D(name, r0, r0 + 8, 128 * b, 128 * b + 128), A("fo", f + 128 * sl, f + 128 * sl + 128, 1, 0, 128, 16)))
+        prs.append((D("ydep", 0, 1, 128 * b, 128 * b + 128), A("fo", f + 896, f + 1024, 1, 0, 1)))
+        dma(prs[:4], "Y", 20000); dma(prs[4:], "S", 20000)
+    yo = A("pb0", 0, 128)
+    mm([(yo, A("idb", 0, 128), A("ghi", 128 * i, 128 * i + 128), i == 0, False) for i in range(16)])
+    mm([(yo, A("idb", 0, 128), A("glo", 128 * i, 128 * i + 128), False, i == 15) for i in range(16)])
+    cp(A("ygs", 0, 128), yo, "VS")
+    dma([(D("yg", 0, 128, 0, 128), A("ygs", 0, 128))], "Y", 1 << 16)
+    return ops
+
+
+def chain(ops, prm):
+    ops = [dict(o) for o in ops]; inst = {}
+    for i, o in enumerate(ops): inst.setdefault(o["n"], []).append(i)
+    for e, names in prm["seq"].items():
+        last = None
+        for t in range(ST):
+            for nme in names:
+                i = inst[nme][t]; ops[i]["alts"] = {e: ops[i]["alts"][e]}
+                if last is not None: ops[i]["deps"] = ops[i]["deps"] | {last}
+                last = i
+    return ops
+
+
+def alts_min(o):
+    return min([a[0] for a in o["alts"].values()] or [0.0])
+
+
+def schedule(ops, prm):
+    n = len(ops); succ = [[] for _ in range(n)]; off, force, win = prm["off"], prm["eng"], prm["win"]
+    for i, o in enumerate(ops):
+        for d in o["deps"]: succ[d].append(i)
+    pr = [0.0] * n; alts = []; cnt = [len(o["deps"]) for o in ops]; topo = [i for i in range(n) if not cnt[i]]
+    for i in topo:
+        for j in succ[i]:
+            cnt[j] -= 1
+            if not cnt[j]: topo.append(j)
+    if len(topo) < n:
+        return None
+    for i in reversed(topo):
+        o = ops[i]; c = min([a[0] for a in o["alts"].values()] or [0.0]) + o["lat"] + (LAT_D if o["kind"] == "d" else 0.0)
+        pr[i] = c + LAT_X + max([pr[j] for j in succ[i]] or [0.0])
+    for i, o in enumerate(ops):
+        bn, tg = o["n"].split(":")
+        pr[i] += 100 * (off.get(o["n"], 0) + off.get(tg, 0) + off.get(bn, 0)) + (prm["small"] if alts_min(o) < 400 else 0)
+        e = force.get(o["n"])
+        alts.append([(x, a[0]) for x, a in o["alts"].items() if e not in o["alts"] or x == e])
+    left = [len(o["deps"]) for o in ops]; ready = {}
+    fin = [0.0] * n; eng = [None] * n; free = {e: 0.0 for e in "VSPGYD"}; bank = {}; order = []; beg = [0.0] * n; more = {}
+
+    def release(i):
+        o = ops[i]
+        if not o["alts"]:
+            fin[i] = beg[i] = max(fin[d] for d in o["deps"]) + o["lat"]; order.append(i); done(i)
+        else:
+            ready[i] = {e: max([0.0] + [fin[d] + ((LAT_S if d in o["raw"] else 0.0) if eng[d] == e else LAT_X) for d in o["deps"]]) for e, c in alts[i]}
+
+    def done(i):
+        for j in succ[i]:
+            left[j] -= 1
+            if not left[j]: release(j)
+
+    for i in [i for i in range(n) if not left[i]]: release(i)
+    while ready:
+        cand = []; lo = 1e18
+        for i, r in ready.items():
+            best = None
+            for e, c in alts[i]:
+                s = max(free[e], r[e])
+                for b in ops[i]["banks"]:
+                    if b in bank: s = max(s, fin[bank[b]] + (0.0 if eng[bank[b]] == e else LAT_X))
+                if best is None or s + c < best[1]: best = (s, s + c, i, e)
+            cand.append(best); lo = min(lo, best[0])
+        s, f, i, e = max([c for c in cand if c[0] <= lo + win], key=lambda c: pr[c[2]])
+        free[e] = f
+        for b in ops[i]["banks"]:
+            if b in bank and eng[bank[b]] != e: more.setdefault(i, []).append(bank[b])
+            bank[b] = i
+        if ops[i]["kind"] == "d":
+            f = free["D"] = max(f + LAT_D, free["D"]) + ops[i]["lat"]
+        fin[i] = f; eng[i] = e; beg[i] = s; order.append(i); del ready[i]
+        done(i)
+    return order, eng, beg, fin, more
+
+
+def place(seq, pred, dur, eng, banks):
+    beg = [0.0] * len(dur); line = {}; held = {}
+    for i in seq:
+        s = 0.0
+        for d, l in pred[i]:
+            x = beg[d] + dur[d] + l
+            if x > s: s = x
+        e = eng[i]; c = dur[i]
+        if e is not None:
+            L = line.setdefault(e, [])
+            while True:
+                lo, hi = 0, len(L)
+                while lo < hi:
+                    m = (lo + hi) // 2
+                    if L[m][1] <= s: lo = m + 1
+                    else: hi = m
+                while lo < len(L) and L[lo][0] < s + c:
+                    s = max(s, L[lo][1]); lo += 1
+                s2 = s
+                for b in banks[i]:
+                    for (x, y, z) in held.get(b, ()):
+                        if z != e and x < s2 + c + LAT_X and s2 < y + LAT_X: s2 = y + LAT_X
+                if s2 == s: break
+                s = s2
+            L.insert(lo, (s, s + c))
+            for b in banks[i]: held.setdefault(b, []).append((s, s + c, e))
+        beg[i] = s
+    return beg
+
+
+def polish(ops, eng, beg, rounds):
+    n = len(ops); E = list(eng); dur = [o["alts"][eng[i]][0] if eng[i] else 0.0 for i, o in enumerate(ops)]
+    banks = [o["banks"] for o in ops]; end = list(range(n)); pred = [[] for _ in range(n)]; beg = list(beg)
+    for i, o in enumerate(ops):
+        if o["kind"] == "d":
+            end[i] = len(dur); dur.append(o["lat"]); E.append("D"); banks.append([]); pred.append([(i, LAT_D)]); beg.append(beg[i] + LAT_D)
+    for i, o in enumerate(ops):
+        for d in o["deps"]:
+            l = o["lat"] if o["kind"] == "a" else ((LAT_S if d in o["raw"] else 0.0) if eng[d] == eng[i] and end[d] == d else LAT_X)
+            pred[i].append((end[d], l))
+    m = len(dur); succ = [[] for _ in range(m)]
+    for i in range(m):
+        for d, l in pred[i]: succ[d].append((i, l))
+    rank = [i if i < n else 0 for i in range(m)]
+    for i in range(n): rank[end[i]] = i + (0.5 if end[i] != i else 0)
+    beg = place(sorted(range(m), key=lambda i: (beg[i], rank[i])), pred, dur, E, banks); best = None
+    for _ in range(rounds + 1):
+        span = max(beg[i] + dur[i] for i in range(m))
+        if best is None or span < best[0]: best = (span, beg)
+        back = place(sorted(range(m), key=lambda i: (-beg[i] - dur[i], -rank[i])), succ, dur, E, banks)
+        beg = place(sorted(range(m), key=lambda i: (-back[i] - dur[i], rank[i])), pred, dur, E, banks)
+    beg = best[1]; order = sorted(range(n), key=lambda i: (beg[i], i)); more = {}; last = {}
+    for i in order:
+        for b in banks[i]:
+            if b in last and eng[last[b]] != eng[i]: more.setdefault(i, []).append(last[b])
+            last[b] = i
+    return order, eng, beg[:n], [beg[end[i]] + dur[end[i]] for i in range(n)], more
+
+
+def arrange(ops, prm):
+    r = schedule(chain(ops, prm), prm)
+    return polish(ops, r[1], r[2], prm["rounds"]) if r else None
+
+
+def plan(prm=PRM):
+    ops = program(prm); order, eng, beg, fin, more = arrange(ops, prm)
+    for i, m in more.items(): ops[i]["deps"].update(m)
+    cnt = {e: 0 for e in ESEM}; mark = {}; known = {e: {} for e in "VSPGY"}; clock = {}; out = []; total = {}; seen = {}
+    for i in order:
+        o = ops[i]; e = eng[i]
+        if o["kind"] == "a":
+            mark[i] = o["x"]; clock[i] = {}; total[o["x"][0]] = o["x"][1]
+            continue
+        kn = known[e]; waits = {}
+        for d in sorted(o["deps"], key=lambda d: -fin[d]):
+            if ops[d]["kind"] == "r" or (eng[d] == e and d not in o["raw"]): continue
+            sem, v = mark[d]
+            if kn.get(sem, 0) < v:
+                waits[sem] = max(waits.get(sem, 0), v); kn[sem] = v; seen[sem] = max(seen.get(sem, 0), v)
+                for s2, v2 in clock[d].items():
+                    if kn.get(s2, 0) < v2: kn[s2] = v2
+        if o["kind"] == "c":
+            cnt[e] += 1; mark[i] = (ESEM[e], cnt[e]); total[ESEM[e]] = cnt[e]
+        elif o["kind"] == "d":
+            mark[i] = o["x"]; total[o["x"][0]] = o["x"][1]
+        else:
+            total["loc"] = total.get("loc", 0) + 8
+        clock[i] = dict(kn)
+        out.append((e, list(waits.items()), o))
+    return out, [(s, v) for s, v in total.items() if seen.get(s, 0) < v], (ops, order, eng, beg, fin)
+
+
+PLAN = []
+
+
+def rank_program(g, core, T, topo):
+    rank = T.rank_of(core)
+    if rank is None:
+        return
+    if not PLAN:
+        PLAN.append(plan())
+    calls, closing, _ = PLAN[0]
+    n = len(T.cores)
+    queue = {"V": g.vector, "S": g.scalar, "P": g.tensor, "G": g, "Y": g.sync}
+    for e, waits, o in calls:
+        for s, v in waits:
+            queue[e].wait_ge(T.sem[s], v)
+        if o["kind"] == "r":
+            src, dst, sem, step, back = o["x"]
+            hop = 1 + step % (n - 1)
+            to = T.cores[(rank - hop) % n if back else (rank + hop) % n]
+            rid, pid = topo.addr(to, core)
+            mask = sum(1 << x for x in topo.engines(core, to)[:8])
+            g.remote_dma(real(T, dst), real(T, src), T.sem[sem], T.sem.loc, pid, rid, mask)
+        elif o["kind"] == "d":
+            o["alts"][e][1](g, T)
+        else:
+            o["alts"][e][1](g, T).then_inc(T.sem[ESEM[e]], 1)
+    for s, v in closing:
+        g.wait_ge(T.sem[s], v)

@@ -4,43 +4,47 @@ from concourse.mybir import dt, AluOpType, AxisListType, ActivationFunctionType
 
 ALU = AluOpType
 ACT = ActivationFunctionType
-ST, NC = 6, 6
+ST, NCM, NBM = 6, 6, 4
 TABW = 32768 + 256
-MW = 256 + 8 * NC
+DW = 2048 + 256
+RW = 2064
+CW = 448
 BF, F32, I32, U16, F16 = "bfloat16", "float32", "int32", "uint16", "float16"
 
 SB = {
-    "tab": (TABW, BF), "gl": (2048, I32), "ghi": (2048, BF), "glo": (2048, BF), "fac": (2048, BF), "zer": (1024, BF),
-    "refw": (264, I32), "cn": (512, BF), "cl": (3 * 512, BF), "cr": (3 * 4096, BF), "nd": (256, I32), "dr": (256, BF),
-    "sin": (128, I32), "sinf": (128, F32), "trn": (128, F32),
-    "pi": (4, I32), "pf": (20, F32), "xcol": (256, F32), "xg": (128, F32), "sel": (144, BF), "go": (144, F16), "one": (144, BF),
-    "goa": (128, F16), "idb": (128, BF), "idh": (128, F16), "tri": (128, BF), "tri2": (128, BF), "tmpc": (128, F32),
-    "m2k": (128, BF), "pick": (768, BF), "pk0": (768, BF), "wa": (64, BF), "w2": (64, BF), "wf": (512, F32), "cc": (48, F16), "ccf": (48, F32),
-    "zc": (272, F16), "dum": (16, F32), "acc": (16, F32), "jh": (144, F32), "sl": (2, U16),
-    "st": (144, F32), "lu": (144, U16), "dh": (48, F32), "g1": (48, F32), "aft": (64, F32),
-    "p3": (64, I32), "we": (48, F32), "wn": (96, I32), "wt": (48, F32), "wl": (48, F32), "wu": (96, F32), "wy": (48, F32),
-    "wm": (48, F32), "wx": (96, F32), "ww": (48, F32), "nb2": (16, F32), "sa": (16, F32), "sc": (16, F32), "jk": (32 * 272, BF), "wen": (48, F32), "w01": (32, F32), "wd": (16, F32),
-    "ra": (768, BF), "o3f": (256, F32), "o3": (256, U16), "o2": (256, U16), "of": (256, U16),
-    "g3": (4096, BF), "g2": (4096, BF), "gt": (4096, BF), "cm": (4096, BF),
-    "sb": (ST * MW, U16), "lb": (ST * MW, U16), "ps": (ST * 16, I32), "pl": (ST * 16, I32),
-    "o32": (256, F32), "bk": (256, F16), "ac": (16, F32), "ac2": (16, F32), "uu": (256, BF), "ohf": (256, BF), "ohk": (256, F16),
-    "xx": (768, F16), "hl": (16, U16), "nb": (16, F32), "kb": (16, F32), "ab": (8 * 272, F32), "nm": (16, F32),
-    "wo": (16, U16), "th": (256, BF), "tl": (256, U16), "tf": (256, F32), "fo": (2 * 1152, F32), "ygs": (128, F32),
+    "tab": (TABW, BF), "gl": (2048, I32), "gh1": (2048, BF), "ghi": (2048, BF), "glo": (2048, BF), "fac": (2048, BF), "ons": (2, BF),
+    "pat": (2048, BF), "pc": (8, F32), "gf": (2048, F16), "idh": (128, F16), "idn": (128, BF), "dw": (2 * DW, BF),
+    "dm": (256, BF), "dv": (512, BF), "sp2": (16, F32), "wd": (512, BF), "yb": (128, F32),
+    "refi": (256, I32), "refw": (RW, F32), "cn": (CW, BF), "cl": (3 * CW, BF), "cr": (3 * 4096, BF), "nd": (256, I32), "ndb": (256, BF), "ndf": (1536, BF),
+    "dtmp": (256, I32), "sin": (256, I32),
+    "pi": (8, I32), "pf": (16, F32), "xcol": (256, F32), "xg": (128, F32), "xlo": (128, F32), "osr": (240, BF), "strip": (240, BF), "rep": (128, BF),
+    "wc": (112, BF), "wcol": (16, F32), "wh": (512, F16), "wb": (256, BF),
+    "sel": (144, BF), "goa": (128, F16), "idb": (128, BF), "tri": (128, BF), "trin": (128, BF), "tmpc": (128, F32),
+    "a1w": (128, F16), "a2w": (128, F16), "a3s": (128, F16), "a3y": (128, F16), "zw": (128, F16),
+    "vsy": (144, F16), "vss": (144, F16), "kw": (144, F16), "aw": (144, F16), "lw": (512, BF),
+    "lc": (NCM * 24, BF), "spr": (16, F32), "cc": (32, BF), "zc": (256, BF), "mh": (32, F32), "ac": (16, F32),
+    "st": (ST * 256, F16), "sr": (ST * 256, F16), "mk": (256, F16), "yy": (256, F16), "lu": (16, U16), "ra": (256, BF),
+    "o3f": (256, F32), "o3": (256, U16), "o2": (256, U16), "of": (256, U16),
+    "g3": (4096, BF), "g2": (4096, BF), "gt": (4096 + 16 * NCM, BF), "cm": (4096, BF),
+    "sb": (ST * 256, U16), "lb": (ST * 256, U16), "xf": (ST * 256, BF), "rp": (ST * 256, BF),
+    "uu": (32, BF), "zz": (64, BF), "fl": (48, U16), "xk": (256, F16), "xh": (256, BF), "xc": (256, BF),
+    "kb": (16, F32), "nb": (16, F32), "nb2": (16, F32), "sa": (16, F32), "sc": (16, F32), "dz": (512, F32), "nm": (16, F32), "wo": (16, U16),
+    "tl": (256, U16), "tf": (256, F32), "oi": (256, I32), "oj": (256, I32), "fo": (256, F32), "ygs": (128, F32),
 }
 SCRATCH = {k: ("sbuf", [128, v[0]], v[1]) for k, v in SB.items()}
 for _b in range(8):
     SCRATCH["pb%d" % _b] = ("psum", [128, 512], F32)
-SEMAPHORES = (["sv", "ss", "sp", "sg", "loc", "yta"] + ["c%d" % i for i in range(3)] + ["b%d" % i for i in range(ST * NC)]
-              + ["p%d" % i for i in range(ST * NC)] + ["d%d" % i for i in range(24)])
+SEMAPHORES = (["sv", "ss", "sp", "sg", "loc", "yta"] + ["c%d" % i for i in range(3)] + ["b%d" % i for i in range(ST * NCM)]
+              + ["p%d" % i for i in range(ST * NBM)] + ["s%d" % i for i in range(ST * NBM)] + ["d%d" % i for i in range(48)])
 ESEM = {"V": "sv", "S": "ss", "P": "sp", "G": "sg"}
 GA, SCA, PEC = 1.56, 3.8, 0.5
 LAT_X, LAT_S, LAT_R, LAT_D = 120.0, 70.0, 2600.0, 2000.0
-PRM = {"ch":[0,64,128,192,256],"split":{"00":2,"01":2,"02":2,"03":2,"10":2,"11":2,"12":2,"13":2,"20":2,"21":2,"22":2,"23":2,"30":2,"31":2,"32":2,"33":2},
-       "off":{"yvp:e1":-47,"cn:s":24,"ygs":-150,"yact:e1":-77,"1x":-83,"gt":77,"yvp":13,"wn":-3,"zer:s":-20,"ra:b1y":90,"zc:s":-9,"wx":0,"yact:e0":80,"yvp:e0":27,"wy":110,"yg":3,"xg:s":-4,"yact":30,"of":-160,"o2":-77,"ps":-10,"xcol:s":10,"ww":-10,"1b":-80},
-       "eng":{"ra:b0":"V","ra:b1":"S","ra:b0y":"S","ra:b1y":"S","ohf:2":"V","fo:e0":"S","nb:3":"S","nb:2":"S","dh:s":"S","fo:e1":"V","th:3":"S","nm:2":"V","nb:0":"S","ohf:0":"V","ygs:e1":"V","nb2:2":"S","nb2:0":"S"},
-       "win":50.0,"both":0,"dfill":3,"small":3000,"uv":[3],
-       "seq":{"V":["g3:0a","g2:0b","g3:2b","g2:1b","g3:3b","g2:2a","g2:3a","gt:0a","cm:0b","cm:0a","cm:1a","cm:1b","cm:2b","cm:2a","cm:3a","cm:3b"],
-              "S":["g3:0b","g3:1b","g3:1a","g2:0a","g3:2a","g2:1a","g3:3a","g2:2b","gt:0b","g2:3b","gt:1a","gt:1b","gt:2a","gt:2b","gt:3a","gt:3b"]},"rounds":4}
+PRM = {"ch": [0, 64, 128, 192, 224, 256], "bt": [0, 128, 256], "vg": [0, 128, 192, 256], "sc": [192, 256], "vc": [14, 15],
+       "split": {"03": 1, "04": 1, "13": 1, "14": 1, "23": 1, "24": 1, "33": 1, "34": 1}, "cut": 2,
+       "off": {"l": -440, "p": 90, "g": 120, "u": -140, "v": -100, "ndb:s": 100, "ndf:s": 100, "pb7:s": 110, "cn:s": 100, "osr:s": 80, "r0": -130, "q": 100, "goa:s": 40, "idb:s": 80, "refw:s": -10, "f": 20, "e1": 370, "1": 40, "r2": 20, "pb1:1": 150, "s": 0, "tab:q": 160, "wh:u": -40, "dw:l": -80, "pb3:s": 30, "pb1:s": 170, "sel:s": 160, "oj:e1": 160, "dm:1": 20, "zw:v": -10, "e0": -110, "zc:v": -10, "yact:e0": -150, "cr:r2": 80, "trin:v": 10, "e": -40, "wcol:v": -40, "a3y:v": 80, "refi:s": 120, "yt:e": 20, "gt:v": 10, "pb5:u": -10, "aw:v": 80, "pb3:1": -80, "mh:v": 80, "glo:s": -120, "wcol:s": -20, "dv:1": -80, "a1w:s": -40, "sp2:l": -20, "wb:u": 40, "wc:v": 0, "gl:s": 10, "tri:v": -10},
+       "eng": {"cr:r1": "SG", "cr:r2": "VS", "ghi:s": "S", "glo:s": "S", "refw:s": "VS", "wcol:v": "V", "wb:u": "S", "cn:s": "V", "wcol:s": "VS", "yb:g": "VS", "cr:r0": "VSG"},
+       "win": 30.0, "dfill": 5, "gfill": 3, "fs": 20, "small": 3000, "acts": [0, 6, 10, 13, 15, 16],
+       "seq": {"V": "o3f:b1 o2:0 o3:b1 g2:0a g3:2a o2:1 st:b1y sb:0 g2:1b o2:2 sb:1 g2:2b o2:3 g3:4a sb:2 gt:0b o2:4 g2:4a sb:3 of:0 cm:0a cm:0b sb:4 of:1 cm:1a cm:1b of:2 cm:2a cm:2b of:3 fl:0 xk:0 cm:3a of:4 cm:4a fl:1 xk:1 xh:1 zz:2 kb:1 xh:0 fl:2 kb:0 xk:2 kb:2 kb:1.1 kb:0.1 dz:2 dz:2.1 sc:2.2 +mk:b0q sc:2.3 nm:w1 +yy:b0q nm:w1.1 sa:2.2 wo:w1 sa:2.3 tab:w0 kb:2.1 +st:b0y nm:w2 +lu:b0 nm:w2.1 +o3f:b0 wo:w2 +o3:b0 tab:w +mk:b1q +yy:b1q +g3:0b +g3:1b +lu:b1", "S": "g2:0b g3:2b g2:1a g3:3a g2:2a g2:3a gt:0a gt:1a gt:1b gt:2b gt:2a gt:3a ac:a1 uu:0 zz:0 gt:4a uu:1 zz:1 xf:0 nb2:0 nb:0 sc:0 sc:0.7 sc:0.2 sc:0.5 sc:0.3 sa:0.5 sc:0.4 sa:0.7 uu:2 sa:0.6 sa:0.1 ac:a0 nb2:1 xf:1 sc:1.1 nb:1 sc:0.1 sc:1.3 xf:2 sa:0.4 sc:0.6 sc:1 sc:1.2 sa:1 sa:1.1 sa:0 sa:1.2 sa:0.2 sa:1.3 nb2:2 sa:0.3 xc:1 nb:2 sc:2 sc:2.1 sa:2 sa:2.1 +ra:b0 xc:2 xh:2 +g3:0a +g3:1a +ra:b1", "P": "pb4:0x.1 pb2:2 pb4:0x.2 pb4:0x.3 pb4:0 pb3:3 pb5:1x pb4:0y pb5:1x.1 pb2:4 pb5:1 pb4:0k pb7:0 pb5:1y pb4:2x pb4:2x.1 pb5:1k pb4:2 pb7:1 pb6:1 pb4:2y pb6:0 pb4:2k pb6:2 +pb0:b0q pb7:2 +pb0:b0y +pb0:b0 +pb1:b0 +pb2:b1q +pb2:b1 +pb3:b1 +pb0:0x +pb1:1x +pb2:b1y +pb0:0 +pb0:2x +pb1:1 +pb1:3x +pb0:2 +pb0:4x +pb1:3 +pb2:0 +pb6:a1 +pb0:4 +pb3:1 +pb6:a0 +pb4:0x", "G": "xf:2> +sb:0> +st:b0y> +st:b1y> +sb:1> +sb:2> +sb:3> +sb:4> +xf:0>"}}
 
 
 def A(n, c0, c1, cs=1, p0=0, p1=128, ps=1):
@@ -77,29 +81,29 @@ def real(T, a):
 
 
 def program(prm):
-    ops, hist, nd, tag = [], {}, [0], ["s"]
-    CH, split = prm["ch"], prm["split"]; NC = len(CH) - 1
-    both = list(range(NC - prm["both"], NC))
+    ops, hist, nd, tag, now, seen = [], {}, [0], ["s"], [-1], {}
+    CH, BT, split = prm["ch"], prm["bt"], prm["split"]; NC = len(CH) - 1; NB = len(BT) - 1
+    CL = [(CH[c], CH[c + 1]) for c in range(NC)]; BL = [(BT[b], BT[b + 1]) for b in range(NB)]; VC = set(prm["vc"])
     PO = [sum(CH[j + 1] - CH[j] for j in range(c % 2, c, 2)) for c in range(NC)]
-    def msg(t, c):
-        return t * MW + CH[c] + 8 * c
+    VG = prm["vg"]; GO = [16 * sum(v < l1 for v in VG[1:-1] if v <= l0) for l0, l1 in CL]
 
     def add(alts, outs, ins, kind="c", lat=0.0, extra=None, after=()):
-        rd, wr = [], []
+        rd, wr, k = [], [], None
         for a in ins:
             if isap(a):
                 rd += [a[1], a[2]] if a[0] == "ind" else [a]
+                if a[0] == "ind": k = "g"
         for a in outs:
             if a[0] == "ind":
-                wr.append(a[1]); rd.append(a[2])
+                wr.append(a[1]); rd.append(a[2]); k = "s"
             else:
                 wr.append(a)
-        me = len(ops); deps = set(after); raw = set(after)
+        me = len(ops); deps = set(after)
         for lst, w in ((rd, False), (wr, True)):
             for a in lst:
                 for (b, o, bw) in hist.get(a[0], ()):
                     if (w or bw) and meet(a[1], b[1]) and meet(a[2], b[2]):
-                        deps.add(o); raw.add(o)
+                        deps.add(o)
         for lst, w in ((rd, False), (wr, True)):
             for a in lst:
                 h = hist.setdefault(a[0], [])
@@ -107,8 +111,11 @@ def program(prm):
                     h[:] = [e for e in h if e[0] != a]
                 h.append((a, me, w))
         banks = sorted(set(a[0] for a in rd + wr if a[0][:2] == "pb"))
-        ops.append({"alts": alts, "deps": deps, "raw": raw, "banks": banks, "kind": kind, "lat": lat, "x": extra,
-                    "n": "%s:%s" % ((wr or rd)[0][0], tag[0])})
+        ops.append({"alts": alts, "deps": deps, "raw": set(deps), "banks": banks, "kind": kind, "lat": lat, "x": extra, "k": k,
+                    "n": "%s:%s" % ((wr or rd)[0][0], tag[0]), "t": now[0]})
+        if now[0] >= 0:
+            nme = ops[me]["n"] + ">" * (kind == "r"); i = seen[now[0], nme] = seen.get((now[0], nme), -1) + 1
+            ops[me]["n"] = nme + (".%d" % i if i else "")
         return me
 
     def two(*aps):
@@ -129,7 +136,6 @@ def program(prm):
         return 75 + GA * ncol(out) if in0[0] == "ind" else max(64.0, 30 + ncol(out))
 
     def e_act(out, in_, f, bias=None, scale=None):
-        kw = {}
         def em(g, T):
             k = {}
             if bias is not None: k["bias"] = real(T, bias)
@@ -143,9 +149,10 @@ def program(prm):
         return lambda g, T: g.vector.tensor_scalar(real(T, out), real(T, in0), real(T, s1), real(T, s2), op0, op1)
 
     def cp(out, in_, eng="V"):
-        alts = {}
+        alts = {}; n = ncol(out)
         if "V" in eng: alts["V"] = (vcost(out, in_), lambda g, T: g.vector.tensor_copy(real(T, out), real(T, in_)))
         if "S" in eng: alts["S"] = (scost(out, in_), e_act(out, in_, ACT.Copy))
+        if "G" in eng: alts["G"] = (170 + 2.0 * n, lambda g, T: g.affine_select(real(T, out), real(T, in_), [[0, n]], ALU.is_ge, 0.0, 0, 0))
         return add(alts, [out], [in_])
 
     def tt(out, a, b, op):
@@ -171,13 +178,17 @@ def program(prm):
             return g.iota(real(T, out), pat, base, cm)
         return add({"G": (150 + 2.0 * ncol(out), em)}, [out], [])
 
-    def mm(lst):
+    def mm(lst, after=()):
         def em(g, T):
             r = None
             for (o, l, rh, s0, s1) in lst:
                 r = g.tensor.matmul(real(T, o), real(T, l), real(T, rh), s0, s1)
             return r
-        return add({"P": (60 + sum(PEC * max(64, ncol(m[2])) for m in lst), em)}, [m[0] for m in lst], [m[1] for m in lst] + [m[2] for m in lst])
+        return add({"P": (60 + sum(PEC * max(min(64, ncol(m[1])), ncol(m[2])) for m in lst), em)},
+                   [m[0] for m in lst], [m[1] for m in lst] + [m[2] for m in lst], after=after)
+
+    def group(lst):
+        return [(o, l, r, i == 0, i == len(lst) - 1) for i, (o, l, r) in enumerate(lst)]
 
     def dma(pairs, q, nbytes):
         sem = "d%d" % nd[0]; nd[0] += 1
@@ -200,313 +211,366 @@ def program(prm):
     def col(n, c):
         return A(n, c, c + 1)
 
-    for h in range(2):
-        dma([(A("gl", 1024 * h, 1024 * h + 1024), D("gloss", 0, 128, 1024 * h, 1024 * h + 1024))], "Y", 1 << 19)
-    ms(A("sin", 0, 128), 0)
-    ms(A("zer", 0, 1024), 0.0)
-    dma([(A("cn", 0, 256), D("cases", 0, 128, 0, 256)), (A("nd", 0, 256, 1, 0, 6), D("need", 0, 6, 0, 256)),
-         (A("nd", 0, 256, 1, 32, 33), D("dep0", 0, 1, 0, 256))], "Y", 70000)
-    prs = []
-    for q in range(7):
-        for g1 in range(2):
-            src = D("vp0", 8 * q + g1, 8 * q + 8, 0, 256, 2) if q < 4 else D("act0", 8 * (q - 4) + g1, 8 * (q - 4) + 8, 0, 256, 2)
-            c0 = (q // 2) * 32 + g1 * 16
-            prs.append((A("sin", c0, c0 + 16, 1, q % 2, 128, 2), src))
-    dma(prs, "Y", 30000)
-    dma([(A("refw", 0, 256), D("refs", 0, 128, 0, 256)), (A("refw", 256, 264), D("refs", 0, 128, 0, 8))], "Y", 1 << 17)
-    dma([(A("fac", 0, 2048), D("facts", 0, 128, 0, 2048))], "Y", 1 << 19)
+    def rows(n, r, c0, c1):
+        return A(n, c0, c1, 1, r, 128, 16)
+
+    dma([(A("dtmp", 0, 256, 1, 0, 1), D("dep0", 0, 1, 0, 256)), (A("nd", 0, 256, 1, 0, 6), D("need", 0, 6, 0, 256))], "S", 8000)
+    for h in range(4):
+        dma([(A("gl", 512 * h, 512 * h + 512), D("gloss", 0, 128, 512 * h, 512 * h + 512))], "Y", 1 << 18)
+    ms(A("ons", 0, 2), 1.0)
+    dma([(A("refi", 0, 256), D("refs", 0, 128, 0, 256)), (A("cn", 0, 256), D("cases", 0, 128, 0, 256))], "S", 3 << 16)
+    add({"G": (140 + 4.0 * 256, lambda g, T: g.partition_broadcast(T.sin[:, 0:256], T.dtmp[0:1, 0:256], 128))}, [A("sin", 0, 256)], [A("dtmp", 0, 256, 1, 0, 1)])
+    dma([(rows("sin", 5, 0, 256), D("vp0", 0, 8, 0, 256))] + [(rows("sin", 9 + j, 0, 256), D("vp0", 8 * j + 8, 8 * j + 16, 0, 256)) for j in range(3)]
+        + [(rows("sin", 6 + j, 0, 256), D("act0", 8 * j, 8 * j + 8, 0, 256)) for j in range(3)], "Y", 60000)
     io(col("pi", 0), [[0, 1]], 0, 1)
-    io(A("xcol", 0, 256), [[1, 256]], 0, 0)
+    for h in range(2):
+        io(A("xcol", 128 * h, 128 * h + 128), [[1, 128]], 128 * h, 0)
     io(A("xg", 0, 128), [[16, 8], [0, 16]], 0, 0)
-    io(A("wa", 0, 64), [[0, 4], [2048, 16]], 0, 0)
-    ts(col("pi", 1), col("pi", 0), 112, None, ALU.bitwise_and)
-    ts(col("pi", 2), col("pi", 0), 15, None, ALU.bitwise_and)
-    ts(col("pi", 3), col("pi", 0), 7, None, ALU.bitwise_and)
-    cp(A("pf", 0, 2), A("pi", 1, 3)); cp(col("pf", 8), col("pi", 0))
-    cp(col("sl", 0), col("pi", 3)); cp(col("sl", 1), col("pi", 3))
-    k = col("pf", 1)
-    ts(col("pf", 2), col("pf", 0), 15.0, None, ALU.add)
-    ts(col("pf", 3), k, 2.0, None, ALU.is_lt)
-    ts(col("pf", 4), k, 16.0, None, ALU.add)
-    ts(col("pf", 5), k, -0.5, -7.0, ALU.mult, ALU.add)
-    ts(col("pf", 9), k, 0.0, 2.0, ALU.is_equal, ALU.mult)
-    tt(col("pf", 6), col("pf", 9), col("pf", 4), ALU.add)
-    ts(col("pf", 7), col("pf", 4), -1.0, None, ALU.mult)
-    ts(A("pf", 16, 20), A("pf", 4, 8), 0.5, None, ALU.mult)
-    ts(A("sel", 0, 144), A("xcol", 0, 144), col("pf", 2), col("pf", 3), ALU.is_equal, ALU.mult)
-    ts(A("idb", 0, 128), A("xcol", 0, 128), col("pf", 8), None, ALU.is_equal)
-    ms(A("one", 0, 144), 0.0); ms(A("one", 15, 144, 16), 1.0)
-    ms(A("m2k", 0, 128), -2048.0)
-    for h in range(2):
-        c = (1024 * h, 1024 * h + 1024)
-        cp(A("ghi", *c), A("gl", *c))
-    for h in range(2):
-        c = (1024 * h, 1024 * h + 1024)
-        tt(A("glo", *c), A("gl", *c), A("ghi", *c), ALU.subtract)
-    tag[0] = "sd"
-    for i in range(prm["dfill"]):
-        dma([(A("tab", TABW - 2048 * (i + 1), TABW - 2048 * i), D("facts", 0, 128, 0, 2048))], "Y", 1 << 19)
+    io(A("xlo", 0, 128), [[0, 8], [1, 16]], 0, 0)
+    for j, m in ((2, 15), (1, 112)):
+        ts(col("pi", j), col("pi", 0), m, None, ALU.bitwise_and)
+        cp(col("pf", j - 1), col("pi", j))
+    cp(col("pf", 3), col("pi", 0))
+    k, p = col("pf", 1), col("pf", 3)
+    tag[0] = "p"
+    ts(col("pc", 4), k, 3.0, 0.0625, ALU.is_equal, ALU.mult)
+    ts(col("pc", 6), k, 4.0, None, ALU.is_ge)
+    ts(A("pat", 0, 128), A("xcol", 0, 128), col("pc", 4), col("pc", 6), ALU.mult, ALU.add)
+    for j in range(4):
+        ts(col("pc", j), k, 2.0, 8.0 * 2 ** j, ALU.is_equal, ALU.mult)
+        ts(A("pat", 128 << j, 256 << j), A("pat", 0, 128 << j), col("pc", j), None, ALU.add)
     tag[0] = "s"
-    for c0 in range(0, TABW - 2048 * prm["dfill"], 1024):
-        o = A("tab", c0, min(TABW - 2048 * prm["dfill"], c0 + 1024)); n = ncol(o)
-        def gfill(g, T, o=o, n=n):
-            return g.iota(real(T, o), [[0, n]], 0, 0, allow_small_or_imprecise_dtypes=True)
-        add({"V": (0.5 * n, lambda g, T, o=o: g.vector.memset(real(T, o), 0.0)), "S": (30 + n, e_act(o, A("zer", 0, n), ACT.Copy)),
-             "G": (150 + 2.0 * n, gfill)}, [o], [A("zer", 0, n)])
-    dma([(A("tab", 0, 32768, 1, 0, 128, 16), A("ghi", 0, 2048))], "Y", 1 << 19)
-    dma([(A("tab", 0, 32768, 1, 1, 128, 16), A("glo", 0, 2048))], "S", 1 << 19)
-    ms(A("cn", 256, 512), 0.0)
-    cp(A("cn", 256, 512, 1, 0, 6), A("nd", 0, 256, 1, 0, 6))
-    cp(A("dr", 0, 256, 1, 32, 33), A("nd", 0, 256, 1, 32, 33))
-    for s in range(3):
-        send(A("cn", 0, 512), A("cl", 512 * s, 512 * s + 512), "c%d" % s, s, False)
-    cp(A("sinf", 0, 128), A("sin", 0, 128), "V")
-    add({"V": (128.0, lambda g, T: g.vector.transpose(T.trn[:], T.sinf[:]))}, [A("trn", 0, 128)], [A("sinf", 0, 128)])
-    mm([(A("pb6", 0, 16), A("one", 15 - lo, 143 - lo, 1, 32, 33), A("dr", lo, 256, 16, 32, 33), lo == 0, lo == 15) for lo in range(16)])
-    def S_(b, s, n=1, buf="st"):
-        return A(buf, 72 * b + 8 * s, 72 * b + 8 * (s + n))
-    def W(n, b, j0=0, j1=3):
-        return A(n, 24 * b + 8 * j0, 24 * b + 8 * j1)
-    io(A("jh", 0, 144), [[1, 6], [-1, 3], [0, 8]], 3, 0)
-    for b in range(2):
-        for q, s in ((0, 0), (6, 1), (5, 2), (4, 3), (3, 4), (2, 5), (1, 6)):
-            c0 = (q // 2) * 32 + q % 2 + 16 * b
-            cp(S_(b, s), A("trn", c0, c0 + 15, 2), "VS")
-        for j in range(3):
-            cp(W("dh", b, j, j + 1), A("pb6", 8 * b, 8 * b + 8), "VS")
-    io(A("w2", 0, 64), [[1024, 4], [-2048, 16]], -2048, 0)
-    ts(A("go", 0, 144), A("xcol", 0, 144), col("pf", 2), None, ALU.is_equal)
+    for j, src, m, a in ((4, 0, 1.0, 15.0), (5, 1, -1.0, 0.0), (6, 1, 16.0, 0.0), (7, 3, 1.0, 112.0), (8, 0, 0.0625, 0.0), (9, 0, 0.0625, 8.0),
+                         (10, 1, -2.0 ** -24, 2.0 ** -25), (11, 1, 1.0 / 32768, 1.0), (12, 1, 2.0 ** -25, -2.0 ** -25), (13, 1, 2.0 ** -25, 0.0), (14, 1, 2048.0, 0.0)):
+        ts(col("pf", j), col("pf", src), m, a, ALU.mult, ALU.add)
+    ts(A("idb", 0, 128), A("xcol", 0, 128), p, None, ALU.is_equal)
+    ts(A("idh", 0, 128), A("xcol", 0, 128), p, None, ALU.is_equal)
+    ts(A("idn", 0, 128), A("xcol", 0, 128), p, -1.0, ALU.is_equal, ALU.mult)
     ts(A("goa", 0, 128), A("xg", 0, 128), col("pf", 0), None, ALU.is_equal)
-    ts(A("idh", 0, 128), A("xcol", 0, 128), col("pf", 8), None, ALU.is_equal)
-    ts(A("tmpc", 0, 128), A("xcol", 0, 128), col("pf", 8), -1.0, ALU.is_gt, ALU.mult)
-    tt(A("tmpc", 0, 128), A("tmpc", 0, 128), A("goa", 0, 128), ALU.mult)
-    ts(A("tri2", 0, 128), A("idb", 0, 128), 16.0, None, ALU.mult)
-    tt(A("tri", 0, 128), A("tri2", 0, 128), A("tmpc", 0, 128), ALU.add)
-    cp(A("tri2", 0, 128), A("tri", 0, 128))
-    ts(A("tmpc", 0, 8), A("idb", 0, 128, 16), 32.0, None, ALU.mult)
-    tt(A("tri2", 0, 128, 16), A("tmpc", 0, 8), A("goa", 0, 128, 16), ALU.subtract)
-    pk0, pk = A("pk0", 0, 768, 1, 0, 32), A("pick", 0, 768, 1, 0, 32)
-    ms(pk0, -1.0)
-    add({"G": (1700.0, lambda g, T: g.affine_select(real(T, pk), real(T, pk0), [[1, 6], [0, 128]], ALU.is_equal, 0.0, 0, -1))}, [pk], [pk0])
-    ts(col("pf", 10), k, 16.0, None, ALU.mult)
-    ts(col("pf", 11), k, -1.0 / 1024, None, ALU.mult)
-    ms(A("ccf", 0, 48), 0.0)
-    for c in range(NC):
-        h0, h1 = CH[c] // 16, CH[c + 1] // 16; nh = h1 - h0
-        ts(A("ccf", 3 * h0 + nh, 3 * h0 + 2 * nh), A("xcol", h0, h1), 1.0 / (64 if c in both else 32), None, ALU.mult)
-        ts(A("ccf", 3 * h0 + 2 * nh, 3 * h0 + 3 * nh), A("xcol", h0, h1), 256.0, col("pf", 10), ALU.mult, ALU.add)
-    cp(A("cc", 0, 48), A("ccf", 0, 48))
-    ts(A("zc", 0, 16), A("xcol", 0, 16), 0.0, col("pf", 11), ALU.mult, ALU.add)
-    ts(col("pf", 12), col("pf", 11), 1.0 / 512, None, ALU.add)
-    ts(A("zc", 16, 272), A("xcol", 0, 256), 1.0 / 512, col("pf", 12), ALU.mult, ALU.add)
-    ts(col("pf", 13), k, 32768.0, None, ALU.add)
-    ts(A("dum", 0, 16), A("xcol", 0, 16), 16.0, col("pf", 13), ALU.mult, ALU.add)
-    ts(A("acc", 0, 16), A("dum", 0, 16), -32766.0, 32768.0, ALU.add, ALU.mult)
-    ts(col("pf", 14), k, 1.0 / 1024, 31.0 / 64, ALU.mult, ALU.add)
-    ts(col("pf", 15), col("pf", 11), -1.0 / 1024, None, ALU.add)
-    io(A("wf", 0, 512), [[0, 2], [1, 256]], 0, 0)
+    ts(A("rep", 0, 128, 1, 0, 16), A("xlo", 0, 128, 1, 0, 16), A("pf", 3, 4, 1, 0, 16), None, ALU.is_equal)
+    io(A("wc", 96, 112, 1, 0, 16), [[0, 16]], 0, 0); io(A("wc", 0, 96, 1, 0, 16), [[0, 96]], 0, 0)
+
+    def put(c0, c1, r, w, cs=1, how="row"):
+        o = A("wc", c0, c1, cs, 0, 16); n = ncol(o)
+        pat, cmp, base, cm = {"row": ([[0, n]], ALU.not_equal, -r, 1), "diag": ([[-1, n]], ALU.not_equal, -r, 1),
+                              "under": ([[0, n]], ALU.is_ge, -r, 1), "from": ([[0, n]], ALU.is_gt, r, -1)}[how]
+        add({"G": (170 + 2.0 * n, lambda g, T: g.affine_select(real(T, o), real(T, o), pat, cmp, float(w), base, cm))}, [o], [o])
+
+    C = {n: 96 + i for i, n in enumerate(("m01", "msk", "ofs", "vs", "a1", "a2", "a3", "c1", "key", "off", "mc", "vy", "ay", "wt", "wx"))}
+    W = {n: col("wcol", c - 96) for n, c in C.items()}
+    one = lambda n, r, w, how="row": put(C[n], C[n] + 1, r, w, 1, how)
+    one("m01", 2, 1, "under"); one("msk", 5, 1, "from"); one("msk", 13, 0, "from")
+    one("ofs", 9, -1024, "from"); one("ofs", 12, 0, "from"); one("ofs", 5, -1024); one("ofs", 13, 1)
+    one("vs", 5, 1); put(C["a1"], C["a3"] + 1, 6, 2048, 1, "diag")
+    mm([(A("pb6", 0, 7), A("rep", 0, 128, 1, 0, 16), A("wc", 96, 103, 1, 0, 16), True, True)])
+    cp(A("wcol", 0, 7), A("pb6", 0, 7), "VS")
+    ts(A("sel", 0, 144), A("xcol", 0, 144), col("pf", 4), W["m01"], ALU.is_equal, ALU.mult)
+    ts(A("vss", 0, 144), A("xcol", 0, 144), col("pf", 4), W["vs"], ALU.is_equal, ALU.mult)
+    for n, c in (("a3s", "a3"), ("a2w", "a2"), ("a1w", "a1")):
+        ts(A(n, 0, 128), A("goa", 0, 128), W[c], None, ALU.mult)
+    for b in range(NB):
+        ts(A("st", *BL[b]), A("sin", *BL[b]), W["msk"], W["ofs"], ALU.mult, ALU.add)
+    cp(A("refw", 0, 256), A("refi", 0, 256))
+    for n in (256, 512, 1024):
+        cp(A("refw", n, 2 * n), A("refw", 0, n), "VS")
+    cp(A("refw", 2048, RW), A("refw", 0, RW - 2048), "VS")
+    for h in range(4):
+        c = (512 * h, 512 * h + 512); ps = A("pb%d" % h, 0, 512)
+        ts(A("gh1", *c), A("gl", *c), 2056.5, None, ALU.add)
+        cp(A("gf", *c), A("gl", *c))
+        ts(A("ghi", *c), A("gh1", *c), -2064.0, None, ALU.add, None, (ACT.Identity, -2064.0))
+        mm(group([(ps, A("idh", 0, 128), A("gf", *c)), (ps, A("idn", 0, 128), A("gh1", *c))]))
+        ts(A("glo", *c), ps, 2064.0, None, ALU.add, None, (ACT.Identity, 2064.0))
+    tag[0] = "f"
+    for i in range(33):
+        o = A("tab", 1024 * i, min(TABW, 1024 * i + 1024)); src = A("pat", 1024 * (i % 2), 1024 * (i % 2) + ncol(o))
+        if i < prm["dfill"]: dma([(o, src)], "Y", 1 << 18)
+        else: ops[cp(o, src, "G" if 32 - prm["gfill"] <= i < 32 else "VS")]["pr"] = -prm["fs"] * i
+    tag[0] = "q"
+    for a0, a1 in zip(prm["acts"], prm["acts"][1:]):
+        dma([(rows("tab", h, 2048 * a, 2048 * a + 2048), rows(("ghi", "glo")[h], a, 0, 2048)) for a in range(a0, a1) for h in range(2)], "Y", (a1 - a0) << 16)
+    tag[0] = "s"; last = len(ops) - 1
+    ops[dma([(A("fac", 0, 2048), D("facts", 0, 128, 0, 2048))], "Y", 1 << 19)]["soft"] = last
+    cp(A("ndb", 0, 256, 1, 0, 6), A("nd", 0, 256, 1, 0, 6))
+    dma([(A("ndf", 0, 1536, 1, 0, 1), A("ndb", 0, 256, 1, 0, 6))], "S", 3000)
+    ms(A("osr", 0, 240, 1, 0, 1), 0.0); ms(A("osr", 112, 128, 1, 0, 1), 1.0)
+    mm(group([(A("pb7", 0, 192), A("osr", 112 - 16 * l, 240 - 16 * l, 1, 0, 1), A("ndf", l, 1536, 8, 0, 1)) for l in range(8)]))
+    ts(A("cn", 256, CW), A("pb7", 0, 192), -1.0, None, ALU.mult, None, (ACT.Copy, None, -1.0))
+    for s in range(3):
+        send(A("cn", 0, CW), A("cl", CW * s, CW * s + CW), "c%d" % s, s, False)
+    tag[0] = "v"
+    for r, w in ((2, 2.0 ** -11), (3, 2.0 ** -11), (4, -8), (12, -2), (13, 8)):
+        one("key", r, w)
+    one("off", 6, 0.0625)
+    one("mc", 2, 1, "from"); one("wt", 15, 1, "under"); put(C["wt"], C["wx"] + 1, 15, 4096)
+    one("c1", 16, 100, "under"); one("c1", 1, 0); one("c1", 14, 0, "from"); one("vy", 5, 1, "under"); one("ay", 7, 2048)
+    mm([(A("pb6", 7, 15), A("rep", 0, 128, 1, 0, 16), A("wc", 103, 111, 1, 0, 16), True, True)])
+    cp(A("wcol", 7, 15), A("pb6", 7, 15), "VS")
+    for n, c in (("kw", "key"), ("aw", "off"), ("vsy", "vy")):
+        ts(A(n, 0, 144), A("xcol", 0, 144), col("pf", 4), W[c], ALU.is_equal, ALU.mult)
+    for n, c in (("zw", "key"), ("a3y", "ay")):
+        ts(A(n, 0, 128), A("goa", 0, 128), W[c], None, ALU.mult)
+    for i, (h, c) in enumerate(((8, "wt"), (9, "wt"), (8, "wx"), (9, "wx"))):
+        ts(A("lw", 128 * i, 128 * i + 128), A("xlo", 0, 128), col("pf", h), W[c], ALU.is_equal, ALU.mult)
+    ts(A("tmpc", 0, 128), A("xcol", 0, 128), p, None, ALU.is_ge)
+    tt(A("tri", 0, 128), A("tmpc", 0, 128), A("goa", 0, 128), ALU.mult)
+    ts(A("trin", 0, 128), A("tri", 0, 128), -1.0, None, ALU.mult)
+    ts(A("spr", 0, 16), A("xcol", 0, 16), 1.0 / 2048, col("pf", 11), ALU.mult, ALU.add)
+    for i in range(2):
+        ts(A("cc", 16 * i, 16 * i + 16), A("xcol", 0, 16), (1 - 2 * i) * 2.0 ** -20, None, ALU.mult)
+    ts(A("zc", 0, 256), A("xcol", 0, 256), 2.0 ** -24, None, ALU.mult)
+    ts(A("mh", 0, 16), A("xcol", 0, 16), -2.0 ** -21, col("pf", 12), ALU.mult, ALU.add)
+    ts(A("mh", 16, 32), A("xcol", 0, 16), 2.0 ** -21, col("pf", 13), ALU.mult, ALU.add)
+    tag[0] = "l"
+    ts(A("sp2", 0, 16), A("spr", 0, 16), -15.0 / 16, None, ALU.add)
+    for i in range(4):
+        ts(col("pc", 7), k, float(i % 2), 1.0 - 2 * (i // 2), ALU.is_equal, ALU.mult)
+        ts(A("wd", 128 * i, 128 * i + 128), A("goa", 0, 128), col("pc", 7), None, ALU.mult)
+    tag[0] = "v"
+    LC = {}
+    for c in range(len(VG) - 1):
+        nh = (VG[c + 1] - VG[c]) // 16; z0 = 16 * (VG[c + 1] + c)
+        if nh not in LC:
+            LC[nh] = A("lc", 24 * len(LC), 24 * len(LC) + 3 * nh); io(LC[nh], [[0, 3], [256, nh]], 0, 0)
+        ms(A("gt", z0, z0 + 16), 0.0)
+    tag[0] = "u"
+    QS, DS, KK, MX, QR, DR = 0, 16, 32, 48, 64, 80
+    put(QS, QS + 16, 12, 1); put(QS + 1, QS + 15, 12, -1, 13)
+    for c0, c1, cs, w in ((1, 15, 13, 2), (3, 7, 3, 2), (2, 6, 3, 1), (15, 16, 1, 1), (4, 8, 3, 3), (8, 12, 3, 4), (9, 13, 3, 5), (10, 14, 3, 6)):
+        put(QS + c0, QS + c1, 13, -w, cs)
+    put(QR, QR + 16, 4, 4); put(QR, QR + 1, 4, -3); put(QR + 5, QR + 8, 4, 1); put(QR + 15, QR + 16, 4, -4)
+    for r in (5, 13):
+        put(DS, DS + 1, r, 1); put(DS + 11, DS + 14 + (r == 13), r, 1)
+    put(DS + 1, DS + 2, 13, -1024); put(DS + 15, DS + 16, 13, -1)
+    put(DS + 2, DS + 5, 9, 1, 1, "diag"); put(DS + 5, DS + 11, 6, -1, 1, "diag")
+    put(DR + 1, DR + 2, 2, 1, 1, "under"); put(DR + 5, DR + 8, 1, 1)
+    put(KK + 6, KK + 14, 6, 1, 1, "diag")
+    put(MX + 5, MX + 6, 5, 1, 1, "under"); put(MX + 6, MX + 12, 5, 1, 1, "diag"); put(MX + 9, MX + 12, 11, 1, 1, "diag"); put(MX + 12, MX + 13, 14, 1, 1, "from")
+    ts(A("strip", 0, 240, 1, 0, 16), A("xcol", 0, 240, 1, 0, 16), A("pf", 7, 8, 1, 0, 16), None, ALU.is_equal)
+    for bank, i0, i1 in (("pb4", 0, 4), ("pb5", 4, 6)):
+        mm([(A(bank, 128 * (i - i0) + 16 * g, 128 * (i - i0) + 16 * g + 16), A("strip", 112 - 16 * g, 240 - 16 * g, 1, 0, 16),
+             A("wc", 16 * i, 16 * i + 16, 1, 0, 16), True, True) for i in range(i0, i1) for g in range(8)])
+    cp(A("wh", 0, 512), A("pb4", 0, 512)); cp(A("wb", 0, 256), A("pb5", 0, 256), "VS")
+    mQS, mDS, mKK, mMX = [A("wh", 128 * i, 128 * i + 128) for i in range(4)]
+    mQR, mDR = A("wb", 0, 128), A("wb", 128, 256)
 
     tabw = A("tab", 0, TABW)
 
-    def update(t, b):
-        p = A("p3", 32 * b, 32 * b + 24); q = 48 * b
-        na, tv, nt = A("wn", q, q + 24), A("wn", q + 24, q + 48), A("wn", q, q + 48)
-        da, x, dx = A("wx", q, q + 24), A("wx", q + 24, q + 48), A("wx", q, q + 48)
-        ua, up, uu = A("wu", q, q + 24), A("wu", q + 24, q + 48), A("wu", q, q + 48)
-        cp(A("p3", 32 * b, 32 * b + 32), IND(A("pl", 16 * t + 8 * b, 16 * t + 8 * b + 8), A("sl", 0, 2)))
-        ts(W("we", b), p, 0.0, None, ALU.is_lt)
-        ts(tv, p, 255, None, ALU.bitwise_and)
-        ts(na, p, 15, None, ALU.bitwise_and)
-        tt(W("wl", b), W("we", b), W("dh", b), ALU.add)
-        tt(dx, nt, S_(b, 1, 6), ALU.subtract)
-        tt(W("wm", b), W("wl", b), A("jh", 24 * t, 24 * t + 24), ALU.is_equal)
-        tt(x, x, W("we", b), ALU.mult)
-        tt(W("wt", b), W("wl", b), W("we", b), ALU.add)
-        tt(W("wy", b), x, W("g1", b), ALU.subtract)
-        tt(ua, da, W("wm", b), ALU.mult)
-        tt(W("wen", b), W("wm", b), W("we", b), ALU.mult)
-        tt(W("ww", b), W("wy", b), W("wm", b), ALU.mult)
-        tt(up, W("wen", b), W("g1", b), ALU.mult)
-        w0, w1 = A("w01", 16 * b, 16 * b + 8), A("w01", 16 * b + 8, 16 * b + 16)
-        tt(w0, W("ww", b, 0, 1), W("ww", b, 1, 2), ALU.add)
-        tt(w1, W("ww", b, 2, 3), A("aft", 32 * b, 32 * b + 8), ALU.add)
-        tt(S_(b, 1, 6), S_(b, 1, 6), uu, ALU.add)
-        tt(S_(b, 0), w0, w1, ALU.add)
-        ts(W("dh", b), W("wt", b), t + 1.0, t + 4.0, ALU.max, ALU.min)
+    def terms(t, b):
+        l = BL[b]; w = l[1] - l[0]; bank = "pb%d" % (2 * (b > 0))
+        s, r = A("st", 256 * t + l[0], 256 * t + l[1]), A("rp", 256 * t + l[0], 256 * t + l[1])
+        q, d = A(bank, 0, w), A(bank, w, 2 * w); tag[0] = "b%dq" % b
+        mm(group([(q, mQS, s), (q, mQR, r)]) + group([(d, mDS, s), (d, mDR, r)]))
+        ts(A("mk", *l), q, W["c1"], 0.0, ALU.min, ALU.is_equal)
+        tt(A("yy", *l), d, A("mk", *l), ALU.mult)
+        return s, A("yy", *l), A(bank, 2 * w, 3 * w)
 
     def lists(t, b):
-        cp(S_(b, 0, 4, "lu"), S_(b, 0, 4))
-        r = 384 * b
-        cp(A("ra", r, r + 128), IND(A("wa", 0, 64), S_(b, 1, 1, "lu")), "VS")
-        o = (128 * b, 128 * b + 128)
-        tt(A("o3f", *o), IND(A("refw", 0, 264), S_(b, 0, 1, "lu")), A("ra", r, r + 128), ALU.add)
-        cp(A("o3", *o), A("o3f", *o))
+        l = BL[b]; w = l[1] - l[0]; h = (l[0] // 16, l[1] // 16)
+        vl = A("pb%d" % (2 * (b > 0)), 496, 496 + w // 16); ra = A("pb%d" % (2 * (b > 0) + 1), 0, w)
+        new = A("st", 256 * t + l[0], 256 * t + l[1])
+        if t:
+            s, y, ps = terms(t - 1, b)
+        tag[0] = "b%d" % b
+        if t:
+            mm(group([(vl, A("vsy", 15 - lo, 143 - lo), A("yy", l[0] + lo, l[1], 16)) for lo in range(16)]))
+            mm(group([(ra, A("a3s", 0, 128), s), (ra, A("a3y", 0, 128), y)]))
+        else:
+            mm(group([(vl, A("vss", 15 - lo, 143 - lo), A("st", l[0] + lo, l[1], 16)) for lo in range(16)]))
+            mm(group([(ra, A("a3s", 0, 128), new)]))
+        ts(A("lu", *h), vl, 1024.0, None, ALU.add)
+        cp(A("ra", *l), ra, "VS")
+        tt(A("o3f", *l), IND(A("refw", 0, RW), A("lu", *h)), A("ra", *l), ALU.add)
+        cp(A("o3", *l), A("o3f", *l))
         tag[0] += "y"
-        cp(A("ra", r + 128, r + 384), IND(A("wa", 0, 64), S_(b, 2, 2, "lu")), "VS")
-        wd = A("wd", 8 * b, 8 * b + 8)
-        ts(wd, W("dh", b, 0, 1), t + 3.0, 32.0, ALU.is_lt, ALU.mult)
-        tt(S_(b, 8), wd, S_(b, 3), ALU.add)
-        for c in range(NC):
-            if CH[c] // 128 == b:
-                w = CH[c + 1] - CH[c]; m = msg(t, c) + w; s0 = 72 * b + 64 + CH[c] % 128 // 16
-                cp(A("sb", m, m + w // 16), A("st", s0, s0 + w // 16))
-        ts(A("aft", 32 * b, 32 * b + 32), IND(S_(b, 0), A("sl", 0, 2)), 1.0, None, ALU.add)
-        tt(W("g1", b), A("aft", 32 * b, 32 * b + 24), S_(b, 4, 3), ALU.subtract)
+        if t:
+            mm(group([(ps, mKK, s), (ps, mMX, y)]))
+            cp(new, ps)
+        send(new, A("sr", 256 * t + l[0], 256 * t + l[1]), "s%d" % (t * NBM + b), t, False)
 
-    def gather(buf, c, off, o0, stage):
-        n = split.get("%d%d" % (stage, c), 1); w = (CH[c + 1] - CH[c]) // n
-        for i in range(n):
-            tag[0] = "%d%s" % (c, "ab"[i] if n > 1 else "")
-            cp(A(buf, 16 * (CH[c] + w * i), 16 * (CH[c] + w * i + w)), IND(tabw, A(off, o0 + w * i, o0 + w * (i + 1))), "VS")
+    def parts(stage, c):
+        n = split.get("%d%d" % (stage, c), prm["cut"]); w = (CL[c][1] - CL[c][0]) // 2
+        cut = [CL[c][0] + 2 * (i * w // n) for i in range(n + 1)]
+        return [("%d%s" % (c, "abcd"[i]), cut[i], cut[i + 1]) for i in range(n)]
+
+    def gather(buf, c, off, o0, stage, b0=0):
+        for nme, u0, u1 in parts(stage, c):
+            tag[0] = nme
+            cp(A(buf, b0 + 16 * u0, b0 + 16 * u1), IND(tabw, A(off, o0 + u0, o0 + u1)), "VS")
         tag[0] = str(c)
 
-    def pick(out, buf, c, first):
-        mm([(out, A("idb", 0, 128), first, True, False)]
-           + [(out, A("sel", 15 - kk, 143 - kk), A(buf, 16 * CH[c] + kk, 16 * CH[c + 1], 16), False, kk == 15) for kk in range(16)])
+    def pick(out, buf, c, first, b0=0):
+        mm(group(([(out,) + first] if first else [])
+                 + [(out, A("sel", 15 - kk, 143 - kk), A(buf, b0 + 16 * CL[c][0] + kk, b0 + 16 * CL[c][1], 16)) for kk in range(16)]))
 
     yts = []
     for t in range(ST):
-        s = t % 3
-        for b in range(2):
-            tag[0] = "b%d" % b
-            if t: update(t - 1, b)
-            lists(t, b)
-        tag[0] = "r%d" % t
+        s = t % 3; m = 256 * t; now[0] = -1; tag[0] = "r%d" % t
         if t < 3:
             for kk in range(16):
-                cp(A("cr", 4096 * s + kk, 4096 * s + 4096, 16), A("cl", 512 * s, 512 * s + 256), "VS")
+                cp(A("cr", 4096 * s + kk, 4096 * s + 4096, 16), A("cl", CW * s, CW * s + 256), "VSG")
+        now[0] = t
+        for b in range(NB):
+            lists(t, b)
         for c in range(NC):
-            l = (CH[c], CH[c + 1]); w = l[1] - l[0]; b = l[0] // 128; r = 384 * b + l[0] % 128; m = msg(t, c)
+            l = CL[c]; w = l[1] - l[0]; lm = (m + l[0], m + l[1])
             bank = "pb%d" % (c % 2); r0 = 2 * PO[c]
-            gather("g3", c, "o3", l[0], 3)
+            gather("g3", c, "o3", 0, 3)
             tag[0] = "%dx" % c
-            pick(A(bank, r0, r0 + w), "g3", c, A("ra", r + 128, r + 128 + w))
+            pick(A(bank, r0, r0 + w), "g3", c, (A("a2w", 0, 128), A("st", *lm)))
             tag[0] = str(c)
             cp(A("o2", *l), A(bank, r0, r0 + w))
-            gather("g2", c, "o2", l[0], 2)
-            pick(A(bank, r0 + w, r0 + 2 * w), "g2", c, A("ra", r + 256, r + 256 + w))
-            cp(A("sb", m, m + w), A(bank, r0 + w, r0 + 2 * w))
-            send(A("sb", m, m + w + w // 16), A("lb", m, m + w + w // 16), "b%d" % (t * NC + c), t, False)
+            gather("g2", c, "o2", 0, 2)
+            pick(A(bank, r0 + w, r0 + 2 * w), "g2", c, (A("a1w", 0, 128), A("st", *lm)))
+            cp(A("sb", *lm), A(bank, r0 + w, r0 + 2 * w))
+            send(A("sb", *lm), A("lb", *lm), "b%d" % (t * NCM + c), t, False)
+        done = 0
+        for b, l in enumerate(BL):
+            tag[0] = "a%d" % b; h = (l[0] // 16, l[1] // 16); ac = A("pb6", 256 + h[0], 256 + h[1])
+            mm(group([(ac, A("idb", 0, 128), A("cc", 16 + h[0], 16 + h[1]))]
+                     + [(ac, A("aw", 15 - lo, 143 - lo), A("sr", m + l[0] + lo, m + l[1], 16)) for lo in range(16 * (t < ST - 1))]))
+            cp(A("ac", *h), ac, "VS")
         for c in range(NC):
-            l = (CH[c], CH[c + 1]); w = l[1] - l[0]; m = msg(t, c); h = (l[0] // 16, l[1] // 16); nh = w // 16
+            l = CL[c]; w = l[1] - l[0]
             pt = A("pb%d" % (2 + c % 2), PO[c], PO[c] + w)
-            vb = "pb%d" % (4 + c % 2); v0 = 3 * PO[c]
-            gather("gt", c, "lb", m, 1)
-            pick(pt, "gt", c, A("m2k", 0, w))
-            ts(A("of", *l), pt, 2048.0, None, ALU.add)
-            n = split.get("0%d" % c, 1)
-            for i in range(n):
-                tag[0] = "%d%s" % (c, "ab"[i] if n > 1 else ""); u = (l[0] + i * w // n, l[0] + (i + 1) * w // n)
-                tt(A("cm", 16 * u[0], 16 * u[1]), IND(A("fac", 0, 2048), A("of", *u)),
-                   A("cr", 4096 * s + 16 * u[0], 4096 * s + 16 * u[1]), ALU.is_le)
+            gather("gt", c, "lb", m, 1, GO[c])
+            pick(pt, "gt", c, None, GO[c])
+            cp(A("of", *l), pt)
+            for nme, u0, u1 in parts(0, c):
+                tag[0] = nme
+                tt(A("cm", 16 * u0, 16 * u1), IND(A("fac", 0, 2048), A("of", u0, u1)), A("cr", 4096 * s + 16 * u0, 4096 * s + 16 * u1), ALU.is_le)
             tag[0] = str(c)
             if t == ST - 1:
                 last = c == NC - 1
                 yts.append(send(A("of", *l), A("tl", *l), "yta", t, True, A("tl", 0, 256) if last else False, yts, NC))
-            cp(A("o32", *l), A("lb", m, m + w))
-            tt(A("bk", *l), IND(A("w2", 0, 64), A("lb", m + w, m + w + nh)), A("o32", *l), ALU.add)
-            ts(A("ac", *h), A("lb", m + w, m + w + nh), 2048.0, 2048.0, ALU.mult, ALU.add)
-            if c in both:
-                tt(A("ac", *h), A("ac", *h), A("acc", *h), ALU.add)
-            cnt, ps, ps2 = A(vb, v0, v0 + w), A(vb, v0 + w, v0 + 2 * w), A(vb, v0 + 2 * w, v0 + 3 * w)
-            n0 = 512 * s + 256 + l[0]
+            if l[1] not in VG:
+                continue
+            go = GO[c]; c = VG.index(l[1]) - 1; l = (VG[c], l[1]); w = l[1] - l[0]; vb = "pb%d" % (4 + c % 2)
+            lm = (m + l[0], m + l[1]); h = (l[0] // 16, l[1] // 16); nh = w // 16; nc = w // 8
+            n0 = CW * s + 256 + 32 * t + l[0] // 8; e = (l[0] // 8, l[1] // 8)
             tag[0] = "%dx" % c
-            mm([(cnt, A("pick", 128 * t, 128 * t + 128, 1, 0, 6), A("cl", n0, n0 + w, 1, 0, 6), True, False)]
-               + [(cnt, A("one", 15 - kk, 143 - kk), A("cm", 16 * l[0] + kk, 16 * l[1], 16), False, kk == 15) for kk in range(16)])
+            lst = group([(A(vb, 0, nc), A("idb", 0, 128), A("cl", n0, n0 + nc))]
+                        + [(A(vb, j, j + 1), A("cm", 16 * l[0] + 128 * j, 16 * l[0] + 128 * j + 128), col("ons", 0)) for j in range(nc)])
+            last = None
+            for j in range(0, nc, 4):
+                last = mm(lst[j + (j > 0):j + 5], [last] if j else [])
             tag[0] = str(c)
-            uv = c in prm["uv"]; e0 = 12 if uv else 0
-            if uv: ts(A("uu", *l), cnt, 0.0, 0.5, ALU.is_lt, ALU.subtract)
-            else: act(A("uu", *l), cnt, ACT.Sign, -0.5, -1.0)
-            mm([(ps2, A("tri2", 0, 128), A("uu", *l), True, True), (ps, A("tri", 0, 128), A("uu", *l), True, True)])
-            x0 = 3 * l[0]
-            ts(A("ohf", *l), ps, col("pf", 4 + e0), None, ALU.is_ge, None, (ACT.Relu, col("pf", 5), 1.0 if uv else 0.5))
-            ts(A("ohk", *l), ps2, col("pf", 6 + e0), None, ALU.is_ge)
-            tt(A("xx", x0 + w, x0 + 2 * w), A("ohk", *l), A("bk", *l), ALU.mult)
-            tt(A("xx", x0, x0 + w), pt, A("ohf", *l), ALU.mult)
-            ts(A("xx", x0 + 2 * w, x0 + 3 * w), ps, col("pf", 7 + e0), k, ALU.is_le, ALU.mult)
-            z0 = 0 if c == 0 else 16 + l[0]; z1 = 16 + l[1]
-            mm([(A("pb7", z0, z1), A("idh", 0, 128), A("zc", z0, z1), True, False),
-                (A("pb7", z1 - w, z1), A("goa", 0, 128), A("xx", x0 + w, x0 + 2 * w), False, True)])
-            q0 = 3 * h[0]
-            pc = A("pb6", q0, q0 + 3 * nh)
-            mm([(pc, A("idh", 0, 128), A("cc", q0, q0 + 3 * nh), True, False)]
-               + [(pc, A("go", 15 - lo, 143 - lo), A("xx", x0 + lo, x0 + 3 * w, 16), False, lo == 15) for lo in range(16)])
-            key = A("pb6", q0 + nh, q0 + 2 * nh)
-            if c in both:
-                ts(A("nb", *h), key, -2.0 ** 25, None, ALU.mult, None, (ACT.Copy, None, -2.0 ** 25))
-            else:
-                ts(A("nb", *h), key, -1.0, col("pf", 14), ALU.mult, ALU.add, (ACT.Identity, col("pf", 14), -1.0))
-                ts(A("nb2", *h), key, -1.0, col("pf", 15), ALU.mult, ALU.add, (ACT.Identity, col("pf", 15), -1.0))
-            pp = (16 * t + h[0], 16 * t + h[1])
-            cp(A("ps", *pp), A("pb6", q0, q0 + nh))
-            if h[1] % 8 == 0:
-                pp = (pp[1] - 8, pp[1])
-                send(A("ps", *pp), A("pl", *pp), "p%d" % (t * NC + c), t, True)
-            cp(A("hl", *h), A("pb6", q0 + 2 * nh, q0 + 3 * nh))
+            act(A("uu", *e), A(vb, 0, nc), ACT.Sign, -0.5, -1.0)
+            mm([(A(vb, 32, 32 + nc), A("trin", 0, 128), A("uu", *e), True, True), (A(vb, 32 + nc, 32 + 2 * nc), A("tri", 0, 128), A("uu", *e), True, True)])
+            z0 = 2 * e[0]
+            ts(A("zz", z0, z0 + 2 * nc), A(vb, 32, 32 + 2 * nc), col("pf", 5), 0.0, ALU.add, ALU.max, (ACT.Relu, col("pf", 5)))
+            lw = lambda i: A("lw", 128 * i, 128 * i + 128)
+            o2, o3 = A(vb, 96, 96 + 2 * nh), A(vb, 96 + 2 * nh, 96 + 3 * nh)
+            tag[0] = "%dy" % c
+            mm(group([(A(vb, 96, 96 + 3 * nh), A("idb", 0, 128), LC[nh])]
+                     + [(o3, lw(i), A("zz", z0 + i % 2 + nc * (i // 2), z0 + nc + nc * (i // 2), 2)) for i in range(4)]
+                     + [(o2, lw(i), A("zz", z0 + i, z0 + 2 * nc, 2)) for i in range(2)]))
+            tag[0] = str(c)
+            f0 = 3 * h[0]; gw = A("gt", 16 * l[0] + go, 16 * l[1] + go + 16)
+            ts(A("fl", f0, f0 + 3 * nh), A(vb, 96, 96 + 3 * nh), col("pf", 6), 16.0 * w, ALU.add, ALU.min)
+            tt(A("xk", *l), IND(gw, A("fl", f0 + 2 * nh, f0 + 3 * nh)), A("sr", *lm), ALU.add)
+            cp(A("xf", *lm), IND(gw, A("fl", f0, f0 + nh)), "VS")
+            if l[1] in BT:
+                b = BT.index(l[1]) - 1; u = (m + BT[b], m + l[1])
+                send(A("xf", *u), A("rp", *u), "p%d" % (t * NBM + b), t, True)
+            ts(A("xh", *l), IND(gw, A("fl", f0 + nh, f0 + 2 * nh)), W["m01"], None, ALU.mult, None, (ACT.Identity, None, W["m01"]))
+            if l[1] in prm["sc"] and t < ST - 1:
+                ts(A("xc", done, l[1]), A("xf", m + done, m + l[1]), W["mc"], None, ALU.mult, None, (ACT.Identity, None, W["mc"]))
+            elif l[1] in prm["sc"]:
+                now[0] = -1; v = (done, l[1]); vm = (m + done, m + l[1]); n = v[1] - v[0]; b1, b3 = "pb1", "pb3"
+                mm(group([(A(b1, 0, n), A("a1w", 0, 128), A("sr", *vm))]))
+                ts(A("dm", *v), A(b1, 0, n), col("pf", 14), None, ALU.is_equal)
+                ps = [A(b3, 128 + n * i, 128 + n * i + n) for i in range(2)]
+                mm(sum([group([(ps[i], A("wd", 128 * i, 128 * i + 128), A("xh", *v)), (ps[i], A("wd", 256 + 128 * i, 384 + 128 * i), A("xf", *vm))])
+                        for i in range(2)], []))
+                for i in range(2):
+                    tt(A("dv", 256 * i + v[0], 256 * i + v[1]), ps[i], A("dm", *v), ALU.mult)
+                now[0] = t
+            key = A(vb, 128, 128 + nh)
+            tag[0] = "%dk" % c
+            mm(group([(key, A("idb", 0, 128), A("cc", *h))] + [(key, A("kw", 15 - lo, 143 - lo), A("xk", l[0] + lo, l[1], 16)) for lo in range(16)]))
+            tag[0] = str(c)
+            for bank, js in (("pb7", set(range(h[0], 16)) - VC), ("pb6", set(range(h[0], 16)) & VC)):
+                if js: mm(group([(A(bank, *l), A("idb", 0, 128), A("zc", *l)), (A(bank, *l), A("zw", 0, 128), A("xk", *l))]))
+            js = [j for j in range(*h) if j not in VC]
+            if js:
+                u = (js[0], js[-1] + 1); ks = A(vb, 128 + u[0] - h[0], 128 + u[1] - h[0])
+                ts(A("nb2", *u), ks, -1.0, col("pf", 10), ALU.mult, ALU.add, (ACT.Identity, col("pf", 10), -1.0))
+                ts(A("nb", *u), ks, -1.0, 31.0 / 2 ** 21, ALU.mult, ALU.add, (ACT.Identity, 31.0 / 2 ** 21, -1.0))
             tt(A("kb", *h), key, A("ac", *h), ALU.add)
+            for bn, an in (("nb2", "sc"), ("nb", "sa")):
+                for j in js:
+                    n = 16 + 16 * j; z = A("pb7", 0, n); bc, acc = col(bn, j), col(an, j); jk = A("g2" if an == "sa" else "g3", 256 * j, 256 * j + n)
+                    add({"S": (50.0 + n, lambda g, T, z=z, jk=jk, bc=bc, acc=acc: g.scalar.activation(
+                        real(T, jk), real(T, z), ACT.Sign, bias=real(T, bc), accum_out=real(T, acc)))}, [acc, jk], [z, bc])
+                if js and an == "sc":
+                    tt(A("kb", *u), A("kb", *u), A("sc", *u), ALU.subtract)
             for j in range(*h):
-                n = 17 + 16 * j; a0 = 272 * (j % 8); ab = A("ab", a0, a0 + n)
-                if c not in both:
-                    for bc, acc in ((col("nb", j), col("sa", j)), (col("nb2", j), col("sc", j))):
-                        z = A("pb7", 15, 15 + n); a0 = 272 * (2 * j + (acc[0] == "sa")); jk = A("jk", a0, a0 + n)
-                        add({"S": (50.0 + n, lambda g, T, z=z, jk=jk, bc=bc, acc=acc: g.scalar.activation(
-                            real(T, jk), real(T, z), ACT.Sign, bias=real(T, bc), accum_out=real(T, acc)))}, [acc, jk], [z, bc])
-                    continue
-                act(ab, A("pb7", 15, 15 + n), ACT.Abs, col("nb", j), 2.0 ** 25)
-                add({"V": (max(64.0, n), lambda g, T, ab=ab, j=j: g.vector.tensor_reduce(real(T, col("nm", j)), real(T, ab), AxisListType.X, ALU.min, negate=True))},
-                    [col("nm", j)], [ab])
-                if c == NC - 1:
-                    ts(col("wo", j), col("nm", j), col("kb", j), col("dum", j), ALU.add, ALU.min)
-            if c >= NC - 2:
-                u = (0, h[1]) if c == NC - 2 else h
-                cp(A("th", 16 * u[0], 16 * u[1]), IND(A("gt", 0, 16 * l[1]), A("hl", *u)), "VS")
-                js = [j for j in range(*u) if max(x for x in range(NC) if CH[x] <= 16 * j) not in both]
-                if js:
-                    v = (js[0], js[-1] + 1)
-                    tt(A("nm", *v), A("sa", *v), A("sc", *v), ALU.subtract)
-                    ts(A("nm", *v), A("nm", *v), 32768.0, None, ALU.mult, None, (ACT.Copy, None, 32768.0))
-                if c == NC - 2 or js:
-                    tt(A("nm", *u), A("nm", *u), A("kb", *u), ALU.add)
-                    tt(A("nm", *u), A("nm", *u), A("dum", *u), ALU.min)
-                    cp(A("wo", *u), A("nm", *u))
-        for c in (NC - 2, NC - 1):
-            tag[0] = str(c); u = (0 if c == NC - 2 else CH[c] // 16, CH[c + 1] // 16)
-            cp(IND(tabw, A("wo", *u)), A("th", 16 * u[0], 16 * u[1]))
-    tag[0] = "e"
-    dma([(A("ghi", 0, 2048), A("tab", 0, 32768, 1, 0, 128, 16))], "Y", 1 << 19)
-    dma([(A("glo", 0, 2048), A("tab", 0, 32768, 1, 1, 128, 16))], "S", 1 << 19)
+                if j in VC:
+                    n = 16 + 16 * j; dz = A("dz", 256 * (j % 2), 256 * (j % 2) + n); r = col("sc", j)
+                    ts(dz, A("pb6", 0, n), col(vb, 128 + j - h[0]), col("mh", j), ALU.subtract, ALU.subtract)
+                    add({"V": (max(64.0, n), lambda g, T, dz=dz, r=r: g.vector.tensor_reduce(
+                        real(T, r), real(T, dz), AxisListType.X, ALU.min, apply_absolute_value=True))}, [r], [dz])
+                    ts(col("sa", j), r, col("mh", 16 + j), 2.0, ALU.is_lt, ALU.mult)
+            if l[1] in prm["sc"]:
+                v = (done, l[1]); u = (done // 16, h[1]); done = l[1]; tag[0] = "w%d" % c
+                tt(A("nm", *u), A("sa", *u), A("kb", *u), ALU.add)
+                tt(A("nm", *u), A("nm", *u), A("spr" if t < ST - 1 else "sp2", *u), ALU.min)
+                ts(A("wo", *u), A("nm", *u), 32768.0, None, ALU.mult)
+        done = 0
+        for i, l1 in enumerate(prm["sc"]):
+            tag[0] = "w" if l1 == 256 else "w%d" % i; v = (done, l1); done = l1
+            wo = A("wo", v[0] // 16, v[1] // 16)
+            if t < ST - 1:
+                tt(IND(tabw, wo), A("xh", *v), A("xc", *v), ALU.add)
+            for j in range(2 * (t == ST - 1)):
+                ops[cp(IND(A("dw", DW * j, DW * j + DW), wo), A("dv", 256 * j + v[0], 256 * j + v[1]))]["n"] = ("tab:", "dw:")[j] + tag[0]
+        if t == 1:
+            now[0] = -1; tag[0] = "l"; last = len(ops) - 1
+            for c0 in range(0, 2 * DW, 288):
+                ops[io(A("dw", c0, c0 + 288), [[0, 288]], 0, 0)]["soft"] = last
+        if t == ST - 2:
+            now[0] = -1; tag[0] = "g"
+            dma([(A("ghi", 0, 2048), rows("tab", 0, 0, 32768))], "Y", 1 << 19)
+            dma([(A("glo", 0, 2048), rows("tab", 1, 0, 32768))], "Y", 1 << 19)
+            for q in range(4):
+                ps = A("pb7", 256 + 128 * (q % 2), 384 + 128 * (q % 2))
+                mm(group([(ps, A("idb", 0, 128), A(("ghi", "glo")[q // 2], 128 * i, 128 * i + 128)) for i in range(8 * (q % 2), 8 * (q % 2) + 8)]))
+                if q: tt(A("yb", 0, 128), ps, A("yb", 0, 128), ALU.add)
+                else: cp(A("yb", 0, 128), ps, "VS")
+    tag[0] = "e"; now[0] = -1
     cp(A("tf", 0, 256), A("tl", 0, 256))
     dma([(D("yt", 0, 128, 0, 256), A("tf", 0, 256))], "Y", 1 << 17)
-    for b in range(2):
-        tag[0] = "e%d" % b
-        update(ST - 1, b)
-        ts(S_(b, 7), W("dh", b, 0, 1), -float(ST), None, ALU.add)
-        cp(S_(b, 0, 8, "lu"), S_(b, 0, 8))
-        f = 1024 * b
-        cp(A("fo", f, f + 512), IND(A("wf", 0, 512), S_(b, 0, 4, "lu")), "VS")
-        cp(A("fo", f + 512, f + 1024), IND(A("wf", 0, 512), S_(b, 4, 4, "lu")), "VS")
-        prs = []
-        for sl, name, r0 in ((0, "yvp", 0), (6, "yvp", 8), (5, "yvp", 16), (4, "yvp", 24), (3, "yact", 0), (2, "yact", 8), (1, "yact", 16)):
-            prs.append((D(name, r0, r0 + 8, 128 * b, 128 * b + 128), A("fo", f + 128 * sl, f + 128 * sl + 128, 1, 0, 128, 16)))
-        prs.append((D("ydep", 0, 1, 128 * b, 128 * b + 128), A("fo", f + 896, f + 1024, 1, 0, 1)))
+    for b in range(NB):
+        l = BL[b]; now[0] = ST
+        s, y, ps = terms(ST - 1, b)
+        tag[0] = "b%dy" % b
+        mm(group([(ps, mKK, s), (ps, mMX, y)]))
+        tag[0] = "e%d" % b; now[0] = -1
+        ts(A("oi", *l), ps, W["ofs"], None, ALU.subtract)
+        ts(A("oj", *l), A("oi", *l), 255, None, ALU.bitwise_and)
+        cp(A("fo", *l), A("oj", *l))
+        prs = [(D("yvp", 0, 8, *l), rows("fo", 5, *l))] + [(D("yvp", 8 * j + 8, 8 * j + 16, *l), rows("fo", 9 + j, *l)) for j in range(3)]
+        prs += [(D("yact", 8 * j, 8 * j + 8, *l), rows("fo", 6 + j, *l)) for j in range(3)] + [(D("ydep", 0, 1, *l), A("fo", l[0], l[1], 1, 12, 13))]
         dma(prs[:4], "Y", 20000); dma(prs[4:], "S", 20000)
     yo = A("pb0", 0, 128)
-    mm([(yo, A("idb", 0, 128), A("ghi", 128 * i, 128 * i + 128), i == 0, False) for i in range(16)])
-    mm([(yo, A("idb", 0, 128), A("glo", 128 * i, 128 * i + 128), False, i == 15) for i in range(16)])
-    cp(A("ygs", 0, 128), yo, "VS")
+    for j in range(2):
+        mm([(yo, A("idb", 0, 128), A("dw", DW * j + 128 * i, DW * j + 128 * i + 128), i + j == 0, i + j == 16) for i in range(16)])
+    tt(A("ygs", 0, 128), yo, A("yb", 0, 128), ALU.add)
     dma([(D("yg", 0, 128, 0, 128), A("ygs", 0, 128))], "Y", 1 << 16)
     return ops
 
 
 def chain(ops, prm):
-    ops = [dict(o) for o in ops]; inst = {}
-    for i, o in enumerate(ops): inst.setdefault(o["n"], []).append(i)
+    ops = [dict(o) for o in ops]; inst = {(o["n"], o["t"]): i for i, o in enumerate(ops) if o["t"] >= 0}
     for e, names in prm["seq"].items():
         last = None
-        for t in range(ST):
-            for nme in names:
-                i = inst[nme][t]; ops[i]["alts"] = {e: ops[i]["alts"][e]}
-                if last is not None: ops[i]["deps"] = ops[i]["deps"] | {last}
+        for t in range(-1, ST + 1):
+            for nme in names.split():
+                i = inst.get((nme.lstrip("+"), t + (nme[0] == "+")))
+                if i is None: continue
+                ops[i]["alts"] = {e: ops[i]["alts"][e]}
+                if last is not None: ops[i]["soft"] = last
                 last = i
     return ops
 
@@ -517,9 +581,10 @@ def alts_min(o):
 
 def schedule(ops, prm):
     n = len(ops); succ = [[] for _ in range(n)]; off, force, win = prm["off"], prm["eng"], prm["win"]
-    for i, o in enumerate(ops):
-        for d in o["deps"]: succ[d].append(i)
-    pr = [0.0] * n; alts = []; cnt = [len(o["deps"]) for o in ops]; topo = [i for i in range(n) if not cnt[i]]
+    pre = [o["deps"] | {o["soft"]} if "soft" in o else o["deps"] for o in ops]
+    for i in range(n):
+        for d in pre[i]: succ[d].append(i)
+    pr = [0.0] * n; alts = []; cnt = [len(x) for x in pre]; topo = [i for i in range(n) if not cnt[i]]
     for i in topo:
         for j in succ[i]:
             cnt[j] -= 1
@@ -531,10 +596,10 @@ def schedule(ops, prm):
         pr[i] = c + LAT_X + max([pr[j] for j in succ[i]] or [0.0])
     for i, o in enumerate(ops):
         bn, tg = o["n"].split(":")
-        pr[i] += 100 * (off.get(o["n"], 0) + off.get(tg, 0) + off.get(bn, 0)) + (prm["small"] if alts_min(o) < 400 else 0)
-        e = force.get(o["n"])
-        alts.append([(x, a[0]) for x, a in o["alts"].items() if e not in o["alts"] or x == e])
-    left = [len(o["deps"]) for o in ops]; ready = {}
+        pr[i] += o.get("pr", 0) + 100 * (off.get(o["n"], 0) + off.get(tg, 0) + off.get(bn, 0)) + (prm["small"] if alts_min(o) < 400 else 0)
+        e = force.get(o["n"], force.get(bn, "VSPGY"))
+        alts.append([(x, a[0]) for x, a in o["alts"].items() if x in e] or [(x, a[0]) for x, a in o["alts"].items()])
+    left = [len(x) for x in pre]; ready = {}
     fin = [0.0] * n; eng = [None] * n; free = {e: 0.0 for e in "VSPGYD"}; bank = {}; order = []; beg = [0.0] * n; more = {}
 
     def release(i):
@@ -632,8 +697,7 @@ def polish(ops, eng, beg, rounds):
 
 
 def arrange(ops, prm):
-    r = schedule(chain(ops, prm), prm)
-    return polish(ops, r[1], r[2], prm["rounds"]) if r else None
+    return schedule(chain(ops, prm), prm)
 
 
 def plan(prm=PRM):

import numpy as np
from concourse.bass import DstId, RemoteDMATransfer
from concourse.mybir import dt, AluOpType, AxisListType, ActivationFunctionType

ALU = AluOpType
ACT = ActivationFunctionType
ST, NCM, NBM = 6, 6, 4
TABW = 32768 + 256
DW = 2048 + 256
RW = 2064
CW = 448
BF, F32, I32, U16, F16 = "bfloat16", "float32", "int32", "uint16", "float16"

SB = {
    "tab": (TABW, BF), "gl": (2048, I32), "gh1": (2048, BF), "ghi": (2048, BF), "glo": (2048, BF), "fac": (2048, BF), "ons": (2, BF),
    "pat": (2048, BF), "pc": (8, F32), "gf": (2048, F16), "idh": (128, F16), "idn": (128, BF), "dw": (2 * DW, BF),
    "dm": (256, BF), "dv": (512, BF), "sp2": (16, F32), "wd": (512, BF), "yb": (128, F32),
    "refi": (256, I32), "refw": (RW, F32), "cn": (CW, BF), "cl": (3 * CW, BF), "cr": (3 * 4096, BF), "nd": (256, I32), "ndb": (256, BF), "ndf": (1536, BF),
    "dtmp": (256, I32), "sin": (256, I32),
    "pi": (8, I32), "pf": (16, F32), "xcol": (256, F32), "xg": (128, F32), "xlo": (128, F32), "osr": (240, BF), "strip": (240, BF), "rep": (128, BF),
    "wc": (112, BF), "wcol": (16, F32), "wh": (512, F16), "wb": (256, BF),
    "sel": (144, BF), "goa": (128, F16), "idb": (128, BF), "tri": (128, BF), "trin": (128, BF), "tmpc": (128, F32),
    "a1w": (128, F16), "a2w": (128, F16), "a3s": (128, F16), "a3y": (128, F16), "zw": (128, F16),
    "vsy": (144, F16), "vss": (144, F16), "kw": (144, F16), "aw": (144, F16), "lw": (512, BF),
    "lc": (NCM * 24, BF), "spr": (16, F32), "cc": (32, BF), "zc": (256, BF), "mh": (32, F32), "ac": (16, F32),
    "st": (ST * 256, F16), "sr": (ST * 256, F16), "mk": (256, F16), "yy": (256, F16), "lu": (16, U16), "ra": (256, BF),
    "o3f": (256, F32), "o3": (256, U16), "o2": (256, U16), "of": (256, U16),
    "g3": (4096, BF), "g2": (4096, BF), "gt": (4096 + 16 * NCM, BF), "cm": (4096, BF),
    "sb": (ST * 256, U16), "lb": (ST * 256, U16), "xf": (ST * 256, BF), "rp": (ST * 256, BF),
    "uu": (32, BF), "zz": (64, BF), "fl": (48, U16), "xk": (256, F16), "xh": (256, BF), "xc": (256, BF),
    "kb": (16, F32), "nb": (16, F32), "nb2": (16, F32), "sa": (16, F32), "sc": (16, F32), "dz": (512, F32), "nm": (16, F32), "wo": (16, U16),
    "tl": (256, U16), "tf": (256, F32), "oi": (256, I32), "oj": (256, I32), "fo": (256, F32), "ygs": (128, F32),
}
SCRATCH = {k: ("sbuf", [128, v[0]], v[1]) for k, v in SB.items()}
for _b in range(8):
    SCRATCH["pb%d" % _b] = ("psum", [128, 512], F32)
SEMAPHORES = (["sv", "ss", "sp", "sg", "loc", "yta"] + ["c%d" % i for i in range(3)] + ["b%d" % i for i in range(ST * NCM)]
              + ["p%d" % i for i in range(ST * NBM)] + ["s%d" % i for i in range(ST * NBM)] + ["d%d" % i for i in range(48)])
ESEM = {"V": "sv", "S": "ss", "P": "sp", "G": "sg"}
GA, SCA, PEC = 1.56, 3.8, 0.5
LAT_X, LAT_S, LAT_R, LAT_D = 120.0, 70.0, 2600.0, 2000.0
PRM = {"ch": [0, 64, 128, 192, 224, 256], "bt": [0, 128, 256], "vg": [0, 128, 192, 256], "sc": [192, 256], "vc": [14, 15],
       "split": {"03": 1, "04": 1, "13": 1, "14": 1, "23": 1, "24": 1, "33": 1, "34": 1}, "cut": 2,
       "off": {"l": -440, "p": 90, "g": 120, "u": -140, "v": -100, "ndb:s": 100, "ndf:s": 100, "pb7:s": 110, "cn:s": 100, "osr:s": 80, "r0": -130, "q": 100, "goa:s": 40, "idb:s": 80, "refw:s": -10, "f": 20, "e1": 370, "1": 40, "r2": 20, "pb1:1": 150, "s": 0, "tab:q": 160, "wh:u": -40, "dw:l": -80, "pb3:s": 30, "pb1:s": 170, "sel:s": 160, "oj:e1": 160, "dm:1": 20, "zw:v": -10, "e0": -110, "zc:v": -10, "yact:e0": -150, "cr:r2": 80, "trin:v": 10, "e": -40, "wcol:v": -40, "a3y:v": 80, "refi:s": 120, "yt:e": 20, "gt:v": 10, "pb5:u": -10, "aw:v": 80, "pb3:1": -80, "mh:v": 80, "glo:s": -120, "wcol:s": -20, "dv:1": -80, "a1w:s": -40, "sp2:l": -20, "wb:u": 40, "wc:v": 0, "gl:s": 10, "tri:v": -10},
       "eng": {"cr:r1": "SG", "cr:r2": "VS", "ghi:s": "S", "glo:s": "S", "refw:s": "VS", "wcol:v": "V", "wb:u": "S", "cn:s": "V", "wcol:s": "VS", "yb:g": "VS", "cr:r0": "VSG"},
       "win": 30.0, "dfill": 5, "gfill": 3, "fs": 20, "small": 3000, "acts": [0, 6, 10, 13, 15, 16],
       "seq": {"V": "o3f:b1 o2:0 o3:b1 g2:0a g3:2a o2:1 st:b1y sb:0 g2:1b o2:2 sb:1 g2:2b o2:3 g3:4a sb:2 gt:0b o2:4 g2:4a sb:3 of:0 cm:0a cm:0b sb:4 of:1 cm:1a cm:1b of:2 cm:2a cm:2b of:3 fl:0 xk:0 cm:3a of:4 cm:4a fl:1 xk:1 xh:1 zz:2 kb:1 xh:0 fl:2 kb:0 xk:2 kb:2 kb:1.1 kb:0.1 dz:2 dz:2.1 sc:2.2 +mk:b0q sc:2.3 nm:w1 +yy:b0q nm:w1.1 sa:2.2 wo:w1 sa:2.3 tab:w0 kb:2.1 +st:b0y nm:w2 +lu:b0 nm:w2.1 +o3f:b0 wo:w2 +o3:b0 tab:w +mk:b1q +yy:b1q +g3:0b +g3:1b +lu:b1", "S": "g2:0b g3:2b g2:1a g3:3a g2:2a g2:3a gt:0a gt:1a gt:1b gt:2b gt:2a gt:3a ac:a1 uu:0 zz:0 gt:4a uu:1 zz:1 xf:0 nb2:0 nb:0 sc:0 sc:0.7 sc:0.2 sc:0.5 sc:0.3 sa:0.5 sc:0.4 sa:0.7 uu:2 sa:0.6 sa:0.1 ac:a0 nb2:1 xf:1 sc:1.1 nb:1 sc:0.1 sc:1.3 xf:2 sa:0.4 sc:0.6 sc:1 sc:1.2 sa:1 sa:1.1 sa:0 sa:1.2 sa:0.2 sa:1.3 nb2:2 sa:0.3 xc:1 nb:2 sc:2 sc:2.1 sa:2 sa:2.1 +ra:b0 xc:2 xh:2 +g3:0a +g3:1a +ra:b1", "P": "pb4:0x.1 pb2:2 pb4:0x.2 pb4:0x.3 pb4:0 pb3:3 pb5:1x pb4:0y pb5:1x.1 pb2:4 pb5:1 pb4:0k pb7:0 pb5:1y pb4:2x pb4:2x.1 pb5:1k pb4:2 pb7:1 pb6:1 pb4:2y pb6:0 pb4:2k pb6:2 +pb0:b0q pb7:2 +pb0:b0y +pb0:b0 +pb1:b0 +pb2:b1q +pb2:b1 +pb3:b1 +pb0:0x +pb1:1x +pb2:b1y +pb0:0 +pb0:2x +pb1:1 +pb1:3x +pb0:2 +pb0:4x +pb1:3 +pb2:0 +pb6:a1 +pb0:4 +pb3:1 +pb6:a0 +pb4:0x", "G": "xf:2> +sb:0> +st:b0y> +st:b1y> +sb:1> +sb:2> +sb:3> +sb:4> +xf:0>"}}


def A(n, c0, c1, cs=1, p0=0, p1=128, ps=1):
    return (n, (p0, p1, ps), (c0, c1, cs))


def IND(win, off):
    return ("ind", win, off)


def isap(x):
    return isinstance(x, tuple)


def ncol(a):
    if a[0] == "ind":
        return 16 * ncol(a[2])
    return len(range(*a[2]))


def meet(r, s):
    if r[1] <= s[0] or s[1] <= r[0]:
        return False
    return not (r[2] == s[2] and r[2] > 1 and (r[0] - s[0]) % r[2])


def real(T, a):
    if not isap(a):
        return a
    if a[0] == "ind":
        return real(T, a[1]).indirect(real(T, a[2]))
    p, c = a[1], a[2]
    return T[a[0]][slice(p[0], p[1], p[2]) if p[2] > 1 else slice(p[0], p[1]), slice(c[0], c[1], c[2]) if c[2] > 1 else slice(c[0], c[1])]


def program(prm):
    ops, hist, nd, tag, now, seen = [], {}, [0], ["s"], [-1], {}
    CH, BT, split = prm["ch"], prm["bt"], prm["split"]; NC = len(CH) - 1; NB = len(BT) - 1
    CL = [(CH[c], CH[c + 1]) for c in range(NC)]; BL = [(BT[b], BT[b + 1]) for b in range(NB)]; VC = set(prm["vc"])
    PO = [sum(CH[j + 1] - CH[j] for j in range(c % 2, c, 2)) for c in range(NC)]
    VG = prm["vg"]; GO = [16 * sum(v < l1 for v in VG[1:-1] if v <= l0) for l0, l1 in CL]

    def add(alts, outs, ins, kind="c", lat=0.0, extra=None, after=()):
        rd, wr, k = [], [], None
        for a in ins:
            if isap(a):
                rd += [a[1], a[2]] if a[0] == "ind" else [a]
                if a[0] == "ind": k = "g"
        for a in outs:
            if a[0] == "ind":
                wr.append(a[1]); rd.append(a[2]); k = "s"
            else:
                wr.append(a)
        me = len(ops); deps = set(after)
        for lst, w in ((rd, False), (wr, True)):
            for a in lst:
                for (b, o, bw) in hist.get(a[0], ()):
                    if (w or bw) and meet(a[1], b[1]) and meet(a[2], b[2]):
                        deps.add(o)
        for lst, w in ((rd, False), (wr, True)):
            for a in lst:
                h = hist.setdefault(a[0], [])
                if w:
                    h[:] = [e for e in h if e[0] != a]
                h.append((a, me, w))
        banks = sorted(set(a[0] for a in rd + wr if a[0][:2] == "pb"))
        ops.append({"alts": alts, "deps": deps, "raw": set(deps), "banks": banks, "kind": kind, "lat": lat, "x": extra, "k": k,
                    "n": "%s:%s" % ((wr or rd)[0][0], tag[0]), "t": now[0]})
        if now[0] >= 0:
            nme = ops[me]["n"] + ">" * (kind == "r"); i = seen[now[0], nme] = seen.get((now[0], nme), -1) + 1
            ops[me]["n"] = nme + (".%d" % i if i else "")
        return me

    def two(*aps):
        return all(a[0] in SB and SB[a[0]][1] in (BF, F16, U16) for a in aps)

    def vcost(out, in0, in1=None):
        if out[0] == "ind":
            return 60 + SCA * ncol(out)
        n = ncol(out)
        if in0[0] == "ind":
            return 60 + GA * n
        c = 2.0 if (in1 is not None and in0[0][:2] != "pb" and in1[0][:2] != "pb") else 1.0
        if two(out, in0) and (in1 is None or two(in1)):
            c *= 0.5
        return max(64.0, c * n)

    def scost(out, in0):
        return 75 + GA * ncol(out) if in0[0] == "ind" else max(64.0, 30 + ncol(out))

    def e_act(out, in_, f, bias=None, scale=None):
        def em(g, T):
            k = {}
            if bias is not None: k["bias"] = real(T, bias)
            if scale is not None: k["scale"] = real(T, scale)
            return g.scalar.activation(real(T, out), real(T, in_), f, **k)
        return em

    def e_ts(out, in0, s1, s2, op0, op1):
        if op1 is None:
            return lambda g, T: g.vector.tensor_scalar(real(T, out), real(T, in0), real(T, s1), None, op0)
        return lambda g, T: g.vector.tensor_scalar(real(T, out), real(T, in0), real(T, s1), real(T, s2), op0, op1)

    def cp(out, in_, eng="V"):
        alts = {}; n = ncol(out)
        if "V" in eng: alts["V"] = (vcost(out, in_), lambda g, T: g.vector.tensor_copy(real(T, out), real(T, in_)))
        if "S" in eng: alts["S"] = (scost(out, in_), e_act(out, in_, ACT.Copy))
        if "G" in eng: alts["G"] = (170 + 2.0 * n, lambda g, T: g.affine_select(real(T, out), real(T, in_), [[0, n]], ALU.is_ge, 0.0, 0, 0))
        return add(alts, [out], [in_])

    def tt(out, a, b, op):
        return add({"V": (vcost(out, a, b), lambda g, T: g.vector.tensor_tensor(real(T, out), real(T, a), real(T, b), op))}, [out], [a, b])

    def ts(out, in0, s1, s2, op0, op1=None, salt=None):
        alts = {"V": (vcost(out, in0), e_ts(out, in0, s1, s2, op0, op1))}
        ins = [in0, s1, s2]
        if salt is not None:
            alts["S"] = (scost(out, in0), e_act(out, in0, *salt)); ins += list(salt[1:])
        return add(alts, [out], ins)

    def act(out, in_, f, bias=None, scale=None):
        return add({"S": (scost(out, in_), e_act(out, in_, f, bias, scale))}, [out], [in_, bias, scale])

    def ms(out, val):
        return add({"V": (max(64.0, ncol(out) * (0.5 if two(out) else 1.0)), lambda g, T: g.vector.memset(real(T, out), val))}, [out], [])

    def io(out, pat, base, cm):
        fl = SB[out[0]][1] != I32
        def em(g, T):
            if fl: return g.iota(real(T, out), pat, base, cm, allow_small_or_imprecise_dtypes=True)
            return g.iota(real(T, out), pat, base, cm)
        return add({"G": (150 + 2.0 * ncol(out), em)}, [out], [])

    def mm(lst, after=()):
        def em(g, T):
            r = None
            for (o, l, rh, s0, s1) in lst:
                r = g.tensor.matmul(real(T, o), real(T, l), real(T, rh), s0, s1)
            return r
        return add({"P": (60 + sum(PEC * max(min(64, ncol(m[1])), ncol(m[2])) for m in lst), em)},
                   [m[0] for m in lst], [m[1] for m in lst] + [m[2] for m in lst], after=after)

    def group(lst):
        return [(o, l, r, i == 0, i == len(lst) - 1) for i, (o, l, r) in enumerate(lst)]

    def dma(pairs, q, nbytes):
        sem = "d%d" % nd[0]; nd[0] += 1
        def em(g, T):
            for (o, i) in pairs:
                (g.sync if q == "Y" else g.scalar).dma_start(real(T, o), real(T, i)).then_inc(T.sem[sem], 16)
        return add({q: (100.0 * len(pairs), em)}, [p[0] for p in pairs], [p[1] for p in pairs], "d", nbytes / 250.0, (sem, 16 * len(pairs)))

    def send(src, dst, sem, step, back, arrive=True, after=(), n=1):
        s = add({"G": (150.0, None)}, [], [src], "r", 0.0, (src, dst, sem, step, back))
        if arrive is True:
            return add({}, [dst], [], "a", LAT_R + 128 * ncol(src) * 2 / 50.0, (sem, 8), after=[s])
        if arrive:
            return add({}, [arrive], [], "a", LAT_R, (sem, 8 * n), after=[s] + list(after))
        return s

    def D(n, r0, r1, c0, c1, rs=1):
        return A(n, c0, c1, 1, r0, r1, rs)

    def col(n, c):
        return A(n, c, c + 1)

    def rows(n, r, c0, c1):
        return A(n, c0, c1, 1, r, 128, 16)

    dma([(A("dtmp", 0, 256, 1, 0, 1), D("dep0", 0, 1, 0, 256)), (A("nd", 0, 256, 1, 0, 6), D("need", 0, 6, 0, 256))], "S", 8000)
    for h in range(4):
        dma([(A("gl", 512 * h, 512 * h + 512), D("gloss", 0, 128, 512 * h, 512 * h + 512))], "Y", 1 << 18)
    ms(A("ons", 0, 2), 1.0)
    dma([(A("refi", 0, 256), D("refs", 0, 128, 0, 256)), (A("cn", 0, 256), D("cases", 0, 128, 0, 256))], "S", 3 << 16)
    add({"G": (140 + 4.0 * 256, lambda g, T: g.partition_broadcast(T.sin[:, 0:256], T.dtmp[0:1, 0:256], 128))}, [A("sin", 0, 256)], [A("dtmp", 0, 256, 1, 0, 1)])
    dma([(rows("sin", 5, 0, 256), D("vp0", 0, 8, 0, 256))] + [(rows("sin", 9 + j, 0, 256), D("vp0", 8 * j + 8, 8 * j + 16, 0, 256)) for j in range(3)]
        + [(rows("sin", 6 + j, 0, 256), D("act0", 8 * j, 8 * j + 8, 0, 256)) for j in range(3)], "Y", 60000)
    io(col("pi", 0), [[0, 1]], 0, 1)
    for h in range(2):
        io(A("xcol", 128 * h, 128 * h + 128), [[1, 128]], 128 * h, 0)
    io(A("xg", 0, 128), [[16, 8], [0, 16]], 0, 0)
    io(A("xlo", 0, 128), [[0, 8], [1, 16]], 0, 0)
    for j, m in ((2, 15), (1, 112)):
        ts(col("pi", j), col("pi", 0), m, None, ALU.bitwise_and)
        cp(col("pf", j - 1), col("pi", j))
    cp(col("pf", 3), col("pi", 0))
    k, p = col("pf", 1), col("pf", 3)
    tag[0] = "p"
    ts(col("pc", 4), k, 3.0, 0.0625, ALU.is_equal, ALU.mult)
    ts(col("pc", 6), k, 4.0, None, ALU.is_ge)
    ts(A("pat", 0, 128), A("xcol", 0, 128), col("pc", 4), col("pc", 6), ALU.mult, ALU.add)
    for j in range(4):
        ts(col("pc", j), k, 2.0, 8.0 * 2 ** j, ALU.is_equal, ALU.mult)
        ts(A("pat", 128 << j, 256 << j), A("pat", 0, 128 << j), col("pc", j), None, ALU.add)
    tag[0] = "s"
    for j, src, m, a in ((4, 0, 1.0, 15.0), (5, 1, -1.0, 0.0), (6, 1, 16.0, 0.0), (7, 3, 1.0, 112.0), (8, 0, 0.0625, 0.0), (9, 0, 0.0625, 8.0),
                         (10, 1, -2.0 ** -24, 2.0 ** -25), (11, 1, 1.0 / 32768, 1.0), (12, 1, 2.0 ** -25, -2.0 ** -25), (13, 1, 2.0 ** -25, 0.0), (14, 1, 2048.0, 0.0)):
        ts(col("pf", j), col("pf", src), m, a, ALU.mult, ALU.add)
    ts(A("idb", 0, 128), A("xcol", 0, 128), p, None, ALU.is_equal)
    ts(A("idh", 0, 128), A("xcol", 0, 128), p, None, ALU.is_equal)
    ts(A("idn", 0, 128), A("xcol", 0, 128), p, -1.0, ALU.is_equal, ALU.mult)
    ts(A("goa", 0, 128), A("xg", 0, 128), col("pf", 0), None, ALU.is_equal)
    ts(A("rep", 0, 128, 1, 0, 16), A("xlo", 0, 128, 1, 0, 16), A("pf", 3, 4, 1, 0, 16), None, ALU.is_equal)
    io(A("wc", 96, 112, 1, 0, 16), [[0, 16]], 0, 0); io(A("wc", 0, 96, 1, 0, 16), [[0, 96]], 0, 0)

    def put(c0, c1, r, w, cs=1, how="row"):
        o = A("wc", c0, c1, cs, 0, 16); n = ncol(o)
        pat, cmp, base, cm = {"row": ([[0, n]], ALU.not_equal, -r, 1), "diag": ([[-1, n]], ALU.not_equal, -r, 1),
                              "under": ([[0, n]], ALU.is_ge, -r, 1), "from": ([[0, n]], ALU.is_gt, r, -1)}[how]
        add({"G": (170 + 2.0 * n, lambda g, T: g.affine_select(real(T, o), real(T, o), pat, cmp, float(w), base, cm))}, [o], [o])

    C = {n: 96 + i for i, n in enumerate(("m01", "msk", "ofs", "vs", "a1", "a2", "a3", "c1", "key", "off", "mc", "vy", "ay", "wt", "wx"))}
    W = {n: col("wcol", c - 96) for n, c in C.items()}
    one = lambda n, r, w, how="row": put(C[n], C[n] + 1, r, w, 1, how)
    one("m01", 2, 1, "under"); one("msk", 5, 1, "from"); one("msk", 13, 0, "from")
    one("ofs", 9, -1024, "from"); one("ofs", 12, 0, "from"); one("ofs", 5, -1024); one("ofs", 13, 1)
    one("vs", 5, 1); put(C["a1"], C["a3"] + 1, 6, 2048, 1, "diag")
    mm([(A("pb6", 0, 7), A("rep", 0, 128, 1, 0, 16), A("wc", 96, 103, 1, 0, 16), True, True)])
    cp(A("wcol", 0, 7), A("pb6", 0, 7), "VS")
    ts(A("sel", 0, 144), A("xcol", 0, 144), col("pf", 4), W["m01"], ALU.is_equal, ALU.mult)
    ts(A("vss", 0, 144), A("xcol", 0, 144), col("pf", 4), W["vs"], ALU.is_equal, ALU.mult)
    for n, c in (("a3s", "a3"), ("a2w", "a2"), ("a1w", "a1")):
        ts(A(n, 0, 128), A("goa", 0, 128), W[c], None, ALU.mult)
    for b in range(NB):
        ts(A("st", *BL[b]), A("sin", *BL[b]), W["msk"], W["ofs"], ALU.mult, ALU.add)
    cp(A("refw", 0, 256), A("refi", 0, 256))
    for n in (256, 512, 1024):
        cp(A("refw", n, 2 * n), A("refw", 0, n), "VS")
    cp(A("refw", 2048, RW), A("refw", 0, RW - 2048), "VS")
    for h in range(4):
        c = (512 * h, 512 * h + 512); ps = A("pb%d" % h, 0, 512)
        ts(A("gh1", *c), A("gl", *c), 2056.5, None, ALU.add)
        cp(A("gf", *c), A("gl", *c))
        ts(A("ghi", *c), A("gh1", *c), -2064.0, None, ALU.add, None, (ACT.Identity, -2064.0))
        mm(group([(ps, A("idh", 0, 128), A("gf", *c)), (ps, A("idn", 0, 128), A("gh1", *c))]))
        ts(A("glo", *c), ps, 2064.0, None, ALU.add, None, (ACT.Identity, 2064.0))
    tag[0] = "f"
    for i in range(33):
        o = A("tab", 1024 * i, min(TABW, 1024 * i + 1024)); src = A("pat", 1024 * (i % 2), 1024 * (i % 2) + ncol(o))
        if i < prm["dfill"]: dma([(o, src)], "Y", 1 << 18)
        else: ops[cp(o, src, "G" if 32 - prm["gfill"] <= i < 32 else "VS")]["pr"] = -prm["fs"] * i
    tag[0] = "q"
    for a0, a1 in zip(prm["acts"], prm["acts"][1:]):
        dma([(rows("tab", h, 2048 * a, 2048 * a + 2048), rows(("ghi", "glo")[h], a, 0, 2048)) for a in range(a0, a1) for h in range(2)], "Y", (a1 - a0) << 16)
    tag[0] = "s"; last = len(ops) - 1
    ops[dma([(A("fac", 0, 2048), D("facts", 0, 128, 0, 2048))], "Y", 1 << 19)]["soft"] = last
    cp(A("ndb", 0, 256, 1, 0, 6), A("nd", 0, 256, 1, 0, 6))
    dma([(A("ndf", 0, 1536, 1, 0, 1), A("ndb", 0, 256, 1, 0, 6))], "S", 3000)
    ms(A("osr", 0, 240, 1, 0, 1), 0.0); ms(A("osr", 112, 128, 1, 0, 1), 1.0)
    mm(group([(A("pb7", 0, 192), A("osr", 112 - 16 * l, 240 - 16 * l, 1, 0, 1), A("ndf", l, 1536, 8, 0, 1)) for l in range(8)]))
    ts(A("cn", 256, CW), A("pb7", 0, 192), -1.0, None, ALU.mult, None, (ACT.Copy, None, -1.0))
    for s in range(3):
        send(A("cn", 0, CW), A("cl", CW * s, CW * s + CW), "c%d" % s, s, False)
    tag[0] = "v"
    for r, w in ((2, 2.0 ** -11), (3, 2.0 ** -11), (4, -8), (12, -2), (13, 8)):
        one("key", r, w)
    one("off", 6, 0.0625)
    one("mc", 2, 1, "from"); one("wt", 15, 1, "under"); put(C["wt"], C["wx"] + 1, 15, 4096)
    one("c1", 16, 100, "under"); one("c1", 1, 0); one("c1", 14, 0, "from"); one("vy", 5, 1, "under"); one("ay", 7, 2048)
    mm([(A("pb6", 7, 15), A("rep", 0, 128, 1, 0, 16), A("wc", 103, 111, 1, 0, 16), True, True)])
    cp(A("wcol", 7, 15), A("pb6", 7, 15), "VS")
    for n, c in (("kw", "key"), ("aw", "off"), ("vsy", "vy")):
        ts(A(n, 0, 144), A("xcol", 0, 144), col("pf", 4), W[c], ALU.is_equal, ALU.mult)
    for n, c in (("zw", "key"), ("a3y", "ay")):
        ts(A(n, 0, 128), A("goa", 0, 128), W[c], None, ALU.mult)
    for i, (h, c) in enumerate(((8, "wt"), (9, "wt"), (8, "wx"), (9, "wx"))):
        ts(A("lw", 128 * i, 128 * i + 128), A("xlo", 0, 128), col("pf", h), W[c], ALU.is_equal, ALU.mult)
    ts(A("tmpc", 0, 128), A("xcol", 0, 128), p, None, ALU.is_ge)
    tt(A("tri", 0, 128), A("tmpc", 0, 128), A("goa", 0, 128), ALU.mult)
    ts(A("trin", 0, 128), A("tri", 0, 128), -1.0, None, ALU.mult)
    ts(A("spr", 0, 16), A("xcol", 0, 16), 1.0 / 2048, col("pf", 11), ALU.mult, ALU.add)
    for i in range(2):
        ts(A("cc", 16 * i, 16 * i + 16), A("xcol", 0, 16), (1 - 2 * i) * 2.0 ** -20, None, ALU.mult)
    ts(A("zc", 0, 256), A("xcol", 0, 256), 2.0 ** -24, None, ALU.mult)
    ts(A("mh", 0, 16), A("xcol", 0, 16), -2.0 ** -21, col("pf", 12), ALU.mult, ALU.add)
    ts(A("mh", 16, 32), A("xcol", 0, 16), 2.0 ** -21, col("pf", 13), ALU.mult, ALU.add)
    tag[0] = "l"
    ts(A("sp2", 0, 16), A("spr", 0, 16), -15.0 / 16, None, ALU.add)
    for i in range(4):
        ts(col("pc", 7), k, float(i % 2), 1.0 - 2 * (i // 2), ALU.is_equal, ALU.mult)
        ts(A("wd", 128 * i, 128 * i + 128), A("goa", 0, 128), col("pc", 7), None, ALU.mult)
    tag[0] = "v"
    LC = {}
    for c in range(len(VG) - 1):
        nh = (VG[c + 1] - VG[c]) // 16; z0 = 16 * (VG[c + 1] + c)
        if nh not in LC:
            LC[nh] = A("lc", 24 * len(LC), 24 * len(LC) + 3 * nh); io(LC[nh], [[0, 3], [256, nh]], 0, 0)
        ms(A("gt", z0, z0 + 16), 0.0)
    tag[0] = "u"
    QS, DS, KK, MX, QR, DR = 0, 16, 32, 48, 64, 80
    put(QS, QS + 16, 12, 1); put(QS + 1, QS + 15, 12, -1, 13)
    for c0, c1, cs, w in ((1, 15, 13, 2), (3, 7, 3, 2), (2, 6, 3, 1), (15, 16, 1, 1), (4, 8, 3, 3), (8, 12, 3, 4), (9, 13, 3, 5), (10, 14, 3, 6)):
        put(QS + c0, QS + c1, 13, -w, cs)
    put(QR, QR + 16, 4, 4); put(QR, QR + 1, 4, -3); put(QR + 5, QR + 8, 4, 1); put(QR + 15, QR + 16, 4, -4)
    for r in (5, 13):
        put(DS, DS + 1, r, 1); put(DS + 11, DS + 14 + (r == 13), r, 1)
    put(DS + 1, DS + 2, 13, -1024); put(DS + 15, DS + 16, 13, -1)
    put(DS + 2, DS + 5, 9, 1, 1, "diag"); put(DS + 5, DS + 11, 6, -1, 1, "diag")
    put(DR + 1, DR + 2, 2, 1, 1, "under"); put(DR + 5, DR + 8, 1, 1)
    put(KK + 6, KK + 14, 6, 1, 1, "diag")
    put(MX + 5, MX + 6, 5, 1, 1, "under"); put(MX + 6, MX + 12, 5, 1, 1, "diag"); put(MX + 9, MX + 12, 11, 1, 1, "diag"); put(MX + 12, MX + 13, 14, 1, 1, "from")
    ts(A("strip", 0, 240, 1, 0, 16), A("xcol", 0, 240, 1, 0, 16), A("pf", 7, 8, 1, 0, 16), None, ALU.is_equal)
    for bank, i0, i1 in (("pb4", 0, 4), ("pb5", 4, 6)):
        mm([(A(bank, 128 * (i - i0) + 16 * g, 128 * (i - i0) + 16 * g + 16), A("strip", 112 - 16 * g, 240 - 16 * g, 1, 0, 16),
             A("wc", 16 * i, 16 * i + 16, 1, 0, 16), True, True) for i in range(i0, i1) for g in range(8)])
    cp(A("wh", 0, 512), A("pb4", 0, 512)); cp(A("wb", 0, 256), A("pb5", 0, 256), "VS")
    mQS, mDS, mKK, mMX = [A("wh", 128 * i, 128 * i + 128) for i in range(4)]
    mQR, mDR = A("wb", 0, 128), A("wb", 128, 256)

    tabw = A("tab", 0, TABW)

    def terms(t, b):
        l = BL[b]; w = l[1] - l[0]; bank = "pb%d" % (2 * (b > 0))
        s, r = A("st", 256 * t + l[0], 256 * t + l[1]), A("rp", 256 * t + l[0], 256 * t + l[1])
        q, d = A(bank, 0, w), A(bank, w, 2 * w); tag[0] = "b%dq" % b
        mm(group([(q, mQS, s), (q, mQR, r)]) + group([(d, mDS, s), (d, mDR, r)]))
        ts(A("mk", *l), q, W["c1"], 0.0, ALU.min, ALU.is_equal)
        tt(A("yy", *l), d, A("mk", *l), ALU.mult)
        return s, A("yy", *l), A(bank, 2 * w, 3 * w)

    def lists(t, b):
        l = BL[b]; w = l[1] - l[0]; h = (l[0] // 16, l[1] // 16)
        vl = A("pb%d" % (2 * (b > 0)), 496, 496 + w // 16); ra = A("pb%d" % (2 * (b > 0) + 1), 0, w)
        new = A("st", 256 * t + l[0], 256 * t + l[1])
        if t:
            s, y, ps = terms(t - 1, b)
        tag[0] = "b%d" % b
        if t:
            mm(group([(vl, A("vsy", 15 - lo, 143 - lo), A("yy", l[0] + lo, l[1], 16)) for lo in range(16)]))
            mm(group([(ra, A("a3s", 0, 128), s), (ra, A("a3y", 0, 128), y)]))
        else:
            mm(group([(vl, A("vss", 15 - lo, 143 - lo), A("st", l[0] + lo, l[1], 16)) for lo in range(16)]))
            mm(group([(ra, A("a3s", 0, 128), new)]))
        ts(A("lu", *h), vl, 1024.0, None, ALU.add)
        cp(A("ra", *l), ra, "VS")
        tt(A("o3f", *l), IND(A("refw", 0, RW), A("lu", *h)), A("ra", *l), ALU.add)
        cp(A("o3", *l), A("o3f", *l))
        tag[0] += "y"
        if t:
            mm(group([(ps, mKK, s), (ps, mMX, y)]))
            cp(new, ps)
        send(new, A("sr", 256 * t + l[0], 256 * t + l[1]), "s%d" % (t * NBM + b), t, False)

    def parts(stage, c):
        n = split.get("%d%d" % (stage, c), prm["cut"]); w = (CL[c][1] - CL[c][0]) // 2
        cut = [CL[c][0] + 2 * (i * w // n) for i in range(n + 1)]
        return [("%d%s" % (c, "abcd"[i]), cut[i], cut[i + 1]) for i in range(n)]

    def gather(buf, c, off, o0, stage, b0=0):
        for nme, u0, u1 in parts(stage, c):
            tag[0] = nme
            cp(A(buf, b0 + 16 * u0, b0 + 16 * u1), IND(tabw, A(off, o0 + u0, o0 + u1)), "VS")
        tag[0] = str(c)

    def pick(out, buf, c, first, b0=0):
        mm(group(([(out,) + first] if first else [])
                 + [(out, A("sel", 15 - kk, 143 - kk), A(buf, b0 + 16 * CL[c][0] + kk, b0 + 16 * CL[c][1], 16)) for kk in range(16)]))

    yts = []
    for t in range(ST):
        s = t % 3; m = 256 * t; now[0] = -1; tag[0] = "r%d" % t
        if t < 3:
            for kk in range(16):
                cp(A("cr", 4096 * s + kk, 4096 * s + 4096, 16), A("cl", CW * s, CW * s + 256), "VSG")
        now[0] = t
        for b in range(NB):
            lists(t, b)
        for c in range(NC):
            l = CL[c]; w = l[1] - l[0]; lm = (m + l[0], m + l[1])
            bank = "pb%d" % (c % 2); r0 = 2 * PO[c]
            gather("g3", c, "o3", 0, 3)
            tag[0] = "%dx" % c
            pick(A(bank, r0, r0 + w), "g3", c, (A("a2w", 0, 128), A("st", *lm)))
            tag[0] = str(c)
            cp(A("o2", *l), A(bank, r0, r0 + w))
            gather("g2", c, "o2", 0, 2)
            pick(A(bank, r0 + w, r0 + 2 * w), "g2", c, (A("a1w", 0, 128), A("st", *lm)))
            cp(A("sb", *lm), A(bank, r0 + w, r0 + 2 * w))
            send(A("sb", *lm), A("lb", *lm), "b%d" % (t * NCM + c), t, False)
        done = 0
        for b, l in enumerate(BL):
            tag[0] = "a%d" % b; h = (l[0] // 16, l[1] // 16); ac = A("pb6", 256 + h[0], 256 + h[1])
            mm(group([(ac, A("idb", 0, 128), A("cc", 16 + h[0], 16 + h[1]))]
                     + [(ac, A("aw", 15 - lo, 143 - lo), A("sr", m + l[0] + lo, m + l[1], 16)) for lo in range(16 * (t < ST - 1))]))
            cp(A("ac", *h), ac, "VS")
        for c in range(NC):
            l = CL[c]; w = l[1] - l[0]
            pt = A("pb%d" % (2 + c % 2), PO[c], PO[c] + w)
            gather("gt", c, "lb", m, 1, GO[c])
            pick(pt, "gt", c, None, GO[c])
            cp(A("of", *l), pt)
            for nme, u0, u1 in parts(0, c):
                tag[0] = nme
                tt(A("cm", 16 * u0, 16 * u1), IND(A("fac", 0, 2048), A("of", u0, u1)), A("cr", 4096 * s + 16 * u0, 4096 * s + 16 * u1), ALU.is_le)
            tag[0] = str(c)
            if t == ST - 1:
                last = c == NC - 1
                yts.append(send(A("of", *l), A("tl", *l), "yta", t, True, A("tl", 0, 256) if last else False, yts, NC))
            if l[1] not in VG:
                continue
            go = GO[c]; c = VG.index(l[1]) - 1; l = (VG[c], l[1]); w = l[1] - l[0]; vb = "pb%d" % (4 + c % 2)
            lm = (m + l[0], m + l[1]); h = (l[0] // 16, l[1] // 16); nh = w // 16; nc = w // 8
            n0 = CW * s + 256 + 32 * t + l[0] // 8; e = (l[0] // 8, l[1] // 8)
            tag[0] = "%dx" % c
            lst = group([(A(vb, 0, nc), A("idb", 0, 128), A("cl", n0, n0 + nc))]
                        + [(A(vb, j, j + 1), A("cm", 16 * l[0] + 128 * j, 16 * l[0] + 128 * j + 128), col("ons", 0)) for j in range(nc)])
            last = None
            for j in range(0, nc, 4):
                last = mm(lst[j + (j > 0):j + 5], [last] if j else [])
            tag[0] = str(c)
            act(A("uu", *e), A(vb, 0, nc), ACT.Sign, -0.5, -1.0)
            mm([(A(vb, 32, 32 + nc), A("trin", 0, 128), A("uu", *e), True, True), (A(vb, 32 + nc, 32 + 2 * nc), A("tri", 0, 128), A("uu", *e), True, True)])
            z0 = 2 * e[0]
            ts(A("zz", z0, z0 + 2 * nc), A(vb, 32, 32 + 2 * nc), col("pf", 5), 0.0, ALU.add, ALU.max, (ACT.Relu, col("pf", 5)))
            lw = lambda i: A("lw", 128 * i, 128 * i + 128)
            o2, o3 = A(vb, 96, 96 + 2 * nh), A(vb, 96 + 2 * nh, 96 + 3 * nh)
            tag[0] = "%dy" % c
            mm(group([(A(vb, 96, 96 + 3 * nh), A("idb", 0, 128), LC[nh])]
                     + [(o3, lw(i), A("zz", z0 + i % 2 + nc * (i // 2), z0 + nc + nc * (i // 2), 2)) for i in range(4)]
                     + [(o2, lw(i), A("zz", z0 + i, z0 + 2 * nc, 2)) for i in range(2)]))
            tag[0] = str(c)
            f0 = 3 * h[0]; gw = A("gt", 16 * l[0] + go, 16 * l[1] + go + 16)
            ts(A("fl", f0, f0 + 3 * nh), A(vb, 96, 96 + 3 * nh), col("pf", 6), 16.0 * w, ALU.add, ALU.min)
            tt(A("xk", *l), IND(gw, A("fl", f0 + 2 * nh, f0 + 3 * nh)), A("sr", *lm), ALU.add)
            cp(A("xf", *lm), IND(gw, A("fl", f0, f0 + nh)), "VS")
            if l[1] in BT:
                b = BT.index(l[1]) - 1; u = (m + BT[b], m + l[1])
                send(A("xf", *u), A("rp", *u), "p%d" % (t * NBM + b), t, True)
            ts(A("xh", *l), IND(gw, A("fl", f0 + nh, f0 + 2 * nh)), W["m01"], None, ALU.mult, None, (ACT.Identity, None, W["m01"]))
            if l[1] in prm["sc"] and t < ST - 1:
                ts(A("xc", done, l[1]), A("xf", m + done, m + l[1]), W["mc"], None, ALU.mult, None, (ACT.Identity, None, W["mc"]))
            elif l[1] in prm["sc"]:
                now[0] = -1; v = (done, l[1]); vm = (m + done, m + l[1]); n = v[1] - v[0]; b1, b3 = "pb1", "pb3"
                mm(group([(A(b1, 0, n), A("a1w", 0, 128), A("sr", *vm))]))
                ts(A("dm", *v), A(b1, 0, n), col("pf", 14), None, ALU.is_equal)
                ps = [A(b3, 128 + n * i, 128 + n * i + n) for i in range(2)]
                mm(sum([group([(ps[i], A("wd", 128 * i, 128 * i + 128), A("xh", *v)), (ps[i], A("wd", 256 + 128 * i, 384 + 128 * i), A("xf", *vm))])
                        for i in range(2)], []))
                for i in range(2):
                    tt(A("dv", 256 * i + v[0], 256 * i + v[1]), ps[i], A("dm", *v), ALU.mult)
                now[0] = t
            key = A(vb, 128, 128 + nh)
            tag[0] = "%dk" % c
            mm(group([(key, A("idb", 0, 128), A("cc", *h))] + [(key, A("kw", 15 - lo, 143 - lo), A("xk", l[0] + lo, l[1], 16)) for lo in range(16)]))
            tag[0] = str(c)
            for bank, js in (("pb7", set(range(h[0], 16)) - VC), ("pb6", set(range(h[0], 16)) & VC)):
                if js: mm(group([(A(bank, *l), A("idb", 0, 128), A("zc", *l)), (A(bank, *l), A("zw", 0, 128), A("xk", *l))]))
            js = [j for j in range(*h) if j not in VC]
            if js:
                u = (js[0], js[-1] + 1); ks = A(vb, 128 + u[0] - h[0], 128 + u[1] - h[0])
                ts(A("nb2", *u), ks, -1.0, col("pf", 10), ALU.mult, ALU.add, (ACT.Identity, col("pf", 10), -1.0))
                ts(A("nb", *u), ks, -1.0, 31.0 / 2 ** 21, ALU.mult, ALU.add, (ACT.Identity, 31.0 / 2 ** 21, -1.0))
            tt(A("kb", *h), key, A("ac", *h), ALU.add)
            for bn, an in (("nb2", "sc"), ("nb", "sa")):
                for j in js:
                    n = 16 + 16 * j; z = A("pb7", 0, n); bc, acc = col(bn, j), col(an, j); jk = A("g2" if an == "sa" else "g3", 256 * j, 256 * j + n)
                    add({"S": (50.0 + n, lambda g, T, z=z, jk=jk, bc=bc, acc=acc: g.scalar.activation(
                        real(T, jk), real(T, z), ACT.Sign, bias=real(T, bc), accum_out=real(T, acc)))}, [acc, jk], [z, bc])
                if js and an == "sc":
                    tt(A("kb", *u), A("kb", *u), A("sc", *u), ALU.subtract)
            for j in range(*h):
                if j in VC:
                    n = 16 + 16 * j; dz = A("dz", 256 * (j % 2), 256 * (j % 2) + n); r = col("sc", j)
                    ts(dz, A("pb6", 0, n), col(vb, 128 + j - h[0]), col("mh", j), ALU.subtract, ALU.subtract)
                    add({"V": (max(64.0, n), lambda g, T, dz=dz, r=r: g.vector.tensor_reduce(
                        real(T, r), real(T, dz), AxisListType.X, ALU.min, apply_absolute_value=True))}, [r], [dz])
                    ts(col("sa", j), r, col("mh", 16 + j), 2.0, ALU.is_lt, ALU.mult)
            if l[1] in prm["sc"]:
                v = (done, l[1]); u = (done // 16, h[1]); done = l[1]; tag[0] = "w%d" % c
                tt(A("nm", *u), A("sa", *u), A("kb", *u), ALU.add)
                tt(A("nm", *u), A("nm", *u), A("spr" if t < ST - 1 else "sp2", *u), ALU.min)
                ts(A("wo", *u), A("nm", *u), 32768.0, None, ALU.mult)
        done = 0
        for i, l1 in enumerate(prm["sc"]):
            tag[0] = "w" if l1 == 256 else "w%d" % i; v = (done, l1); done = l1
            wo = A("wo", v[0] // 16, v[1] // 16)
            if t < ST - 1:
                tt(IND(tabw, wo), A("xh", *v), A("xc", *v), ALU.add)
            for j in range(2 * (t == ST - 1)):
                ops[cp(IND(A("dw", DW * j, DW * j + DW), wo), A("dv", 256 * j + v[0], 256 * j + v[1]))]["n"] = ("tab:", "dw:")[j] + tag[0]
        if t == 1:
            now[0] = -1; tag[0] = "l"; last = len(ops) - 1
            for c0 in range(0, 2 * DW, 288):
                ops[io(A("dw", c0, c0 + 288), [[0, 288]], 0, 0)]["soft"] = last
        if t == ST - 2:
            now[0] = -1; tag[0] = "g"
            dma([(A("ghi", 0, 2048), rows("tab", 0, 0, 32768))], "Y", 1 << 19)
            dma([(A("glo", 0, 2048), rows("tab", 1, 0, 32768))], "Y", 1 << 19)
            for q in range(4):
                ps = A("pb7", 256 + 128 * (q % 2), 384 + 128 * (q % 2))
                mm(group([(ps, A("idb", 0, 128), A(("ghi", "glo")[q // 2], 128 * i, 128 * i + 128)) for i in range(8 * (q % 2), 8 * (q % 2) + 8)]))
                if q: tt(A("yb", 0, 128), ps, A("yb", 0, 128), ALU.add)
                else: cp(A("yb", 0, 128), ps, "VS")
    tag[0] = "e"; now[0] = -1
    cp(A("tf", 0, 256), A("tl", 0, 256))
    dma([(D("yt", 0, 128, 0, 256), A("tf", 0, 256))], "Y", 1 << 17)
    for b in range(NB):
        l = BL[b]; now[0] = ST
        s, y, ps = terms(ST - 1, b)
        tag[0] = "b%dy" % b
        mm(group([(ps, mKK, s), (ps, mMX, y)]))
        tag[0] = "e%d" % b; now[0] = -1
        ts(A("oi", *l), ps, W["ofs"], None, ALU.subtract)
        ts(A("oj", *l), A("oi", *l), 255, None, ALU.bitwise_and)
        cp(A("fo", *l), A("oj", *l))
        prs = [(D("yvp", 0, 8, *l), rows("fo", 5, *l))] + [(D("yvp", 8 * j + 8, 8 * j + 16, *l), rows("fo", 9 + j, *l)) for j in range(3)]
        prs += [(D("yact", 8 * j, 8 * j + 8, *l), rows("fo", 6 + j, *l)) for j in range(3)] + [(D("ydep", 0, 1, *l), A("fo", l[0], l[1], 1, 12, 13))]
        dma(prs[:4], "Y", 20000); dma(prs[4:], "S", 20000)
    yo = A("pb0", 0, 128)
    for j in range(2):
        mm([(yo, A("idb", 0, 128), A("dw", DW * j + 128 * i, DW * j + 128 * i + 128), i + j == 0, i + j == 16) for i in range(16)])
    tt(A("ygs", 0, 128), yo, A("yb", 0, 128), ALU.add)
    dma([(D("yg", 0, 128, 0, 128), A("ygs", 0, 128))], "Y", 1 << 16)
    return ops


def chain(ops, prm):
    ops = [dict(o) for o in ops]; inst = {(o["n"], o["t"]): i for i, o in enumerate(ops) if o["t"] >= 0}
    for e, names in prm["seq"].items():
        last = None
        for t in range(-1, ST + 1):
            for nme in names.split():
                i = inst.get((nme.lstrip("+"), t + (nme[0] == "+")))
                if i is None: continue
                ops[i]["alts"] = {e: ops[i]["alts"][e]}
                if last is not None: ops[i]["soft"] = last
                last = i
    return ops


def alts_min(o):
    return min([a[0] for a in o["alts"].values()] or [0.0])


def schedule(ops, prm):
    n = len(ops); succ = [[] for _ in range(n)]; off, force, win = prm["off"], prm["eng"], prm["win"]
    pre = [o["deps"] | {o["soft"]} if "soft" in o else o["deps"] for o in ops]
    for i in range(n):
        for d in pre[i]: succ[d].append(i)
    pr = [0.0] * n; alts = []; cnt = [len(x) for x in pre]; topo = [i for i in range(n) if not cnt[i]]
    for i in topo:
        for j in succ[i]:
            cnt[j] -= 1
            if not cnt[j]: topo.append(j)
    if len(topo) < n:
        return None
    for i in reversed(topo):
        o = ops[i]; c = min([a[0] for a in o["alts"].values()] or [0.0]) + o["lat"] + (LAT_D if o["kind"] == "d" else 0.0)
        pr[i] = c + LAT_X + max([pr[j] for j in succ[i]] or [0.0])
    for i, o in enumerate(ops):
        bn, tg = o["n"].split(":")
        pr[i] += o.get("pr", 0) + 100 * (off.get(o["n"], 0) + off.get(tg, 0) + off.get(bn, 0)) + (prm["small"] if alts_min(o) < 400 else 0)
        e = force.get(o["n"], force.get(bn, "VSPGY"))
        alts.append([(x, a[0]) for x, a in o["alts"].items() if x in e] or [(x, a[0]) for x, a in o["alts"].items()])
    left = [len(x) for x in pre]; ready = {}
    fin = [0.0] * n; eng = [None] * n; free = {e: 0.0 for e in "VSPGYD"}; bank = {}; order = []; beg = [0.0] * n; more = {}

    def release(i):
        o = ops[i]
        if not o["alts"]:
            fin[i] = beg[i] = max(fin[d] for d in o["deps"]) + o["lat"]; order.append(i); done(i)
        else:
            ready[i] = {e: max([0.0] + [fin[d] + ((LAT_S if d in o["raw"] else 0.0) if eng[d] == e else LAT_X) for d in o["deps"]]) for e, c in alts[i]}

    def done(i):
        for j in succ[i]:
            left[j] -= 1
            if not left[j]: release(j)

    for i in [i for i in range(n) if not left[i]]: release(i)
    while ready:
        cand = []; lo = 1e18
        for i, r in ready.items():
            best = None
            for e, c in alts[i]:
                s = max(free[e], r[e])
                for b in ops[i]["banks"]:
                    if b in bank: s = max(s, fin[bank[b]] + (0.0 if eng[bank[b]] == e else LAT_X))
                if best is None or s + c < best[1]: best = (s, s + c, i, e)
            cand.append(best); lo = min(lo, best[0])
        s, f, i, e = max([c for c in cand if c[0] <= lo + win], key=lambda c: pr[c[2]])
        free[e] = f
        for b in ops[i]["banks"]:
            if b in bank and eng[bank[b]] != e: more.setdefault(i, []).append(bank[b])
            bank[b] = i
        if ops[i]["kind"] == "d":
            f = free["D"] = max(f + LAT_D, free["D"]) + ops[i]["lat"]
        fin[i] = f; eng[i] = e; beg[i] = s; order.append(i); del ready[i]
        done(i)
    return order, eng, beg, fin, more


def place(seq, pred, dur, eng, banks):
    beg = [0.0] * len(dur); line = {}; held = {}
    for i in seq:
        s = 0.0
        for d, l in pred[i]:
            x = beg[d] + dur[d] + l
            if x > s: s = x
        e = eng[i]; c = dur[i]
        if e is not None:
            L = line.setdefault(e, [])
            while True:
                lo, hi = 0, len(L)
                while lo < hi:
                    m = (lo + hi) // 2
                    if L[m][1] <= s: lo = m + 1
                    else: hi = m
                while lo < len(L) and L[lo][0] < s + c:
                    s = max(s, L[lo][1]); lo += 1
                s2 = s
                for b in banks[i]:
                    for (x, y, z) in held.get(b, ()):
                        if z != e and x < s2 + c + LAT_X and s2 < y + LAT_X: s2 = y + LAT_X
                if s2 == s: break
                s = s2
            L.insert(lo, (s, s + c))
            for b in banks[i]: held.setdefault(b, []).append((s, s + c, e))
        beg[i] = s
    return beg


def polish(ops, eng, beg, rounds):
    n = len(ops); E = list(eng); dur = [o["alts"][eng[i]][0] if eng[i] else 0.0 for i, o in enumerate(ops)]
    banks = [o["banks"] for o in ops]; end = list(range(n)); pred = [[] for _ in range(n)]; beg = list(beg)
    for i, o in enumerate(ops):
        if o["kind"] == "d":
            end[i] = len(dur); dur.append(o["lat"]); E.append("D"); banks.append([]); pred.append([(i, LAT_D)]); beg.append(beg[i] + LAT_D)
    for i, o in enumerate(ops):
        for d in o["deps"]:
            l = o["lat"] if o["kind"] == "a" else ((LAT_S if d in o["raw"] else 0.0) if eng[d] == eng[i] and end[d] == d else LAT_X)
            pred[i].append((end[d], l))
    m = len(dur); succ = [[] for _ in range(m)]
    for i in range(m):
        for d, l in pred[i]: succ[d].append((i, l))
    rank = [i if i < n else 0 for i in range(m)]
    for i in range(n): rank[end[i]] = i + (0.5 if end[i] != i else 0)
    beg = place(sorted(range(m), key=lambda i: (beg[i], rank[i])), pred, dur, E, banks); best = None
    for _ in range(rounds + 1):
        span = max(beg[i] + dur[i] for i in range(m))
        if best is None or span < best[0]: best = (span, beg)
        back = place(sorted(range(m), key=lambda i: (-beg[i] - dur[i], -rank[i])), succ, dur, E, banks)
        beg = place(sorted(range(m), key=lambda i: (-back[i] - dur[i], rank[i])), pred, dur, E, banks)
    beg = best[1]; order = sorted(range(n), key=lambda i: (beg[i], i)); more = {}; last = {}
    for i in order:
        for b in banks[i]:
            if b in last and eng[last[b]] != eng[i]: more.setdefault(i, []).append(last[b])
            last[b] = i
    return order, eng, beg[:n], [beg[end[i]] + dur[end[i]] for i in range(n)], more


def arrange(ops, prm):
    return schedule(chain(ops, prm), prm)


def plan(prm=PRM):
    ops = program(prm); order, eng, beg, fin, more = arrange(ops, prm)
    for i, m in more.items(): ops[i]["deps"].update(m)
    cnt = {e: 0 for e in ESEM}; mark = {}; known = {e: {} for e in "VSPGY"}; clock = {}; out = []; total = {}; seen = {}
    for i in order:
        o = ops[i]; e = eng[i]
        if o["kind"] == "a":
            mark[i] = o["x"]; clock[i] = {}; total[o["x"][0]] = o["x"][1]
            continue
        kn = known[e]; waits = {}
        for d in sorted(o["deps"], key=lambda d: -fin[d]):
            if ops[d]["kind"] == "r" or (eng[d] == e and d not in o["raw"]): continue
            sem, v = mark[d]
            if kn.get(sem, 0) < v:
                waits[sem] = max(waits.get(sem, 0), v); kn[sem] = v; seen[sem] = max(seen.get(sem, 0), v)
                for s2, v2 in clock[d].items():
                    if kn.get(s2, 0) < v2: kn[s2] = v2
        if o["kind"] == "c":
            cnt[e] += 1; mark[i] = (ESEM[e], cnt[e]); total[ESEM[e]] = cnt[e]
        elif o["kind"] == "d":
            mark[i] = o["x"]; total[o["x"][0]] = o["x"][1]
        else:
            total["loc"] = total.get("loc", 0) + 8
        clock[i] = dict(kn)
        out.append((e, list(waits.items()), o))
    return out, [(s, v) for s, v in total.items() if seen.get(s, 0) < v], (ops, order, eng, beg, fin)


PLAN = []


def rank_program(g, core, T, topo):
    rank = T.rank_of(core)
    if rank is None:
        return
    if not PLAN:
        PLAN.append(plan())
    calls, closing, _ = PLAN[0]
    n = len(T.cores)
    queue = {"V": g.vector, "S": g.scalar, "P": g.tensor, "G": g, "Y": g.sync}
    for e, waits, o in calls:
        for s, v in waits:
            queue[e].wait_ge(T.sem[s], v)
        if o["kind"] == "r":
            src, dst, sem, step, back = o["x"]
            hop = 1 + step % (n - 1)
            to = T.cores[(rank - hop) % n if back else (rank + hop) % n]
            rid, pid = topo.addr(to, core)
            mask = sum(1 << x for x in topo.engines(core, to)[:8])
            g.remote_dma(real(T, dst), real(T, src), T.sem[sem], T.sem.loc, pid, rid, mask)
        elif o["kind"] == "d":
            o["alts"][e][1](g, T)
        else:
            o["alts"][e][1](g, T).then_inc(T.sem[ESEM[e]], 1)
    for s, v in closing:
        g.wait_ge(T.sem[s], v)
